import numpy as np, ml_dtypes
CORES = [25,29,65,69,153,157,193,197]
N = 8
BF = ml_dtypes.bfloat16
def f(rng, *shape):
    return (rng.standard_normal(shape, dtype=np.float32) * np.exp2(rng.integers(-2, 3, shape[:-1] + (1,)))).astype(BF)
def wide(rng, *shape):
    v = f(rng, *shape).astype(np.float32); k = shape[:-2] + (1, shape[-1])
    return (v * np.exp2(rng.integers(-6, 7, k)) * (rng.random(k) > 0.0625)).astype(BF)
R, W, S, C = 8, 128, 3, 1
H = N * R
ROW, COL = np.arange(H)[None, :, None], np.arange(W)[None, None, :]
def stored(v):
    return np.ascontiguousarray(v.reshape(8, N, R, W).transpose(1, 0, 2, 3)).reshape(N, 8, R * W).astype(np.int32)
def whole(v):
    return np.ascontiguousarray(v.reshape(N, 8, R, W).transpose(1, 0, 2, 3)).reshape(8, H, W).astype(np.int64)
def field(rng):
    d = np.repeat(np.repeat(rng.integers(-1, 2, (2, 8, H // 8, W // 16)), 8, axis=2), 16, axis=3)
    d = np.roll(d, int(rng.integers(1, 8)), axis=2)
    return np.where(rng.random(d.shape) < 0.125, rng.integers(-1, 2, d.shape), d)
def inputs_of(rng, v):
    return {"vy": stored(v[0]), "vx": stored(v[1]), "img": f(rng, N, 128, C * R * W)}
def setup_inputs(rng):
    return inputs_of(rng, field(rng))
def setup_inputs_far(rng):
    v = np.zeros((2, 8, H, W), np.int64); o = rng.permutation(8)
    for k in range(8):
        v[0, o[k]] = 1 if k & 1 else -1; v[1, o[k]] = 1 if k & 2 else -1
        if k >= 4:
            m = rng.random((2, H, W)) < 0.015625
            v[:, o[k]] = np.where(m, rng.integers(-1, 2, (2, H, W)), v[:, o[k]])
    return inputs_of(rng, v)
def setup_inputs_ends(rng):
    v = field(rng); pm = np.array([-1, 1])
    for e in (0, H - 1): v[0, :, e, :] = rng.choice(pm, (8, W))
    for e in (0, W - 1): v[1, :, :, e] = rng.choice(pm, (8, H))
    v[0, :, 1, :] = np.where(rng.random((8, W)) < 0.75, -1, 1); v[0, :, H - 2, :] = np.where(rng.random((8, W)) < 0.75, 1, -1)
    v[1, :, :, 1] = np.where(rng.random((8, H)) < 0.75, -1, 1); v[1, :, :, W - 2] = np.where(rng.random((8, H)) < 0.75, 1, -1)
    o = rng.permutation(8); g, h = o[0], o[1]
    v[0, g, 0, :] = 2 * (np.arange(W) & 1) - 1; v[1, g, 0, :] = 1
    v[0, g, H - 1, :] = 2 * (np.arange(W) & 1) - 1; v[1, g, H - 1, :] = -1
    v[1, h, :, 0] = 2 * (np.arange(H) & 1) - 1; v[0, h, :, 0] = 1
    v[1, h, :, W - 1] = 2 * (np.arange(H) & 1) - 1; v[0, h, :, W - 1] = -1
    return inputs_of(rng, v)
def setup_inputs_sinks(rng):
    v = np.zeros((2, 8, H, W), np.int64); o = rng.permutation(8)
    v[1, o[1]] = 1 - 2 * (COL[0] & 1)
    v[0, o[2]] = 2 * (ROW[0] & 1) - 1
    for k in range(3, 8):
        r0, c0 = int(rng.integers(0, H)), int(rng.integers(0, W))
        if k == 3: r0 = R * int(rng.integers(1, N))
        if k == 4: r0 = R * int(rng.integers(1, N)) - 1
        v[0, o[k]] = np.sign(r0 - ROW[0]); v[1, o[k]] = np.sign(c0 - COL[0])
    return inputs_of(rng, v)
def setup_inputs_spread(rng):
    d = setup_inputs(rng); d["img"] = wide(rng, N, 128, C * R * W); return d
def check_inputs(d):
    bad = [k for k in ("vy", "vx") if not np.isin(np.asarray(d[k]), [-1, 0, 1]).all()]
    return bad + ([] if np.isfinite(np.asarray(d["img"]).astype(np.float32)).all() else ["finite"])
def place(a, b):
    return np.minimum(np.maximum(ROW + a, 0), H - 1), (COL + b) % W
def reference(vy, vx, img):
    a, b = whole(vy), whole(vx); g = np.arange(8)[:, None, None]
    for s in range(S):
        p, q = place(a, b)
        a, b = a + a[g, p, q], b + b[g, p, q]
    p, q = place(a, b)
    u = np.ascontiguousarray(img.reshape(N, 8, 16, C, R, W).transpose(1, 0, 4, 5, 2, 3)).reshape(8, H, W, 16, C)
    z = u[g, p, q].reshape(8, N, R, W, 16, C)
    return {"y": np.ascontiguousarray(z.transpose(1, 0, 4, 5, 2, 3)).reshape(N, 128, C * R * W)}

@@ -1,0 +1,340 @@
+from concourse.bass import DstId, RemoteDMATransfer
+from concourse.mybir import AluOpType as A, ActivationFunctionType as F
+
+BF, F32, I32, U16 = "bfloat16", "float32", "int32", "uint16"
+SCRATCH = {
+    "vyi": ("sbuf", [128, 4, 16], I32), "vxi": ("sbuf", [128, 4, 16], I32), "ci": ("sbuf", [128, 4, 16], I32),
+    "xiota": ("sbuf", [128, 4, 16], I32), "pidx": ("sbuf", [128, 1], I32), "qi": ("sbuf", [128, 1], I32),
+    "oi": ("sbuf", [128, 1], I32), "rowc": ("sbuf", [128, 1], F32), "odd": ("sbuf", [128, 1], F32),
+    "even": ("sbuf", [128, 1], F32), "mi": ("sbuf", [128, 1], I32), "kcol": ("sbuf", [128, 8], F32),
+    "dig": ("sbuf", [128, 8, 16], BF), "dnear": ("sbuf", [128, 8, 16], BF), "dfar": ("sbuf", [128, 8, 16], BF),
+    "t1": ("sbuf", [128, 4, 16], F32), "gg": ("sbuf", [128, 4, 16], F32),
+    "blk": ("sbuf", [128, 4, 32], F32), "tb": ("sbuf", [128, 4, 32], F32), "lf": ("sbuf", [128, 64], F32),
+    "l0": ("sbuf", [128, 192], U16), "l1": ("sbuf", [128, 192], U16), "l2": ("sbuf", [128, 64], U16),
+    "l3": ("sbuf", [128, 64], U16),
+    "li": ("sbuf", [128, 64], I32), "la": ("sbuf", [128, 64], I32), "lb": ("sbuf", [128, 64], I32),
+    "w0": ("sbuf", [128, 3072], BF), "w1": ("sbuf", [128, 3072], BF), "w2": ("sbuf", [128, 3072], BF),
+    "w3": ("sbuf", [128, 1024], BF), "pic": ("sbuf", [128, 3072], BF), "yo": ("sbuf", [128, 1024], BF),
+    "sel": ("sbuf", [128, 144], BF),
+    "rv": ("sbuf", [128, 8, 16], BF), "rp": ("sbuf", [128, 512], BF), "rq": ("sbuf", [128, 256], BF),
+    "pn": ("psum", [128, 512], F32), "pf": ("psum", [128, 512], F32),
+    "p2": ("psum", [128, 512], F32), "p3": ("psum", [128, 512], F32),
+}
+SEMAPHORES = ["vc", "gi", "ldv", "ldi", "ms", "sb", "sel1", "sel2", "dg", "rs_o", "rs_n", "rs_f", "lo", "ln", "lfar",
+              "g_e", "g_n", "g_f", "h_n", "h_f", "g_2", "g_3v", "g_3s", "t_n", "t_f", "t_2", "t_3",
+              "c_n", "c_f", "c_2", "c_3", "vir0", "vir1", "vir2",
+              "vn", "vf", "pnr", "pfr", "sent", "sty_a", "sty_b", "rva", "rpa", "rsent"]
+
+
+def plan(T, topo):
+    cs = list(T.cores)
+    near, far, flows = {}, {}, []
+    for a, b in zip(cs, cs[1:]):
+        if b in topo.cores_of(a):
+            near[a], near[b] = b, a
+        else:
+            far[a], far[b] = b, a
+            flows += [(a, b), (b, a)]
+    relays = {}
+    for s, d in flows:
+        own = [f for f in flows if f[0] in topo.cores_of(s)]
+        k = own.index((s, d))
+        c = [x for x in topo.cores_of(s) if T.rank_of(x) is None and topo.may_write(x, d)]
+        if len(own) > 1:
+            by = [[x for x in c if topo.die(x) == e] for e in (0, 1)]
+            c = [y[k] for y in by]
+        relays[(s, d)] = sorted(c, key=lambda x: (topo.die(x) != topo.die(s), x))
+    return near, far, relays
+
+
+def bits(engines):
+    m = 0
+    for e in engines:
+        m |= 1 << e
+    return m
+
+
+def transfer(topo, src, dst, out, in_, engines, sem):
+    rid, pid = topo.addr(dst, src)
+    return RemoteDMATransfer(dst_ids=[DstId(rid=rid, pnc=pid)], dma_engine_mask=bits(engines), remote_sem=sem,
+                             src=in_, dst=out)
+
+
+def rank_program(g, core, T, topo):
+    near, far, relays = plan(T, topo)
+    sem = T.sem
+    if T.rank_of(core) is None:
+        for (s, d), rel in relays.items():
+            if core in rel:
+                hand_on(g, core, T, topo, s, d, rel)
+        return
+    r, n = T.rank_of(core), len(T.cores)
+    nb, fb = near[core], far.get(core)
+    up = T.rank_of(nb) > r
+    edge = fb is None
+    V, S, TE, SY = g.vector, g.scalar, g.tensor, g.sync
+    top = 8 * r - 8
+    cnt = [0, 0]
+
+    def v(ins, name=None):
+        if name:
+            ins.then_inc(sem[name], 1)
+        else:
+            ins.then_inc(sem.vc, 1)
+            cnt[0] += 1
+
+    def vs():
+        if cnt[0] > cnt[1]:
+            V.wait_ge(sem.vc, cnt[0])
+            cnt[1] = cnt[0]
+
+    def ts(out, in0, s1, op0, s2=None, op1=None):
+        if op1 is None:
+            return V.tensor_scalar(out=out, in0=in0, scalar1=s1, scalar2=None, op0=op0)
+        return V.tensor_scalar(out=out, in0=in0, scalar1=s1, scalar2=s2, op0=op0, op1=op1)
+
+    SY.dma_start(out=T.vyi[:], in_=T.vy[:]).then_inc(sem.ldv, 16)
+    S.dma_start(out=T.vxi[:], in_=T.vx[:]).then_inc(sem.ldv, 16)
+    SY.dma_start(out=T.pic[:, 1024:1536], in_=T.img[:, 0:512]).then_inc(sem.ldi, 16)
+    S.dma_start(out=T.pic[:, 1536:2048], in_=T.img[:, 512:1024]).then_inc(sem.ldi, 16)
+
+    g.iota(out=T.pidx[:], pattern=[[1, 1]], base=0, channel_multiplier=1).then_inc(sem.gi, 1)
+    g.iota(out=T.xiota[:], pattern=[[16, 4], [1, 16]], base=0, channel_multiplier=64).then_inc(sem.gi, 1)
+    v(V.memset(T.sel[:], 128.0), "sb")
+    V.wait_ge(sem.gi, 2)
+    v(ts(T.qi[:], T.pidx[:], 15, A.bitwise_and, 1, A.arith_shift_right))
+    v(ts(T.oi[:], T.pidx[:], 4, A.arith_shift_right, 1, A.bitwise_and))
+    if edge:
+        v(ts(T.mi[:], T.pidx[:], 15, A.bitwise_and))
+    vs()
+    v(ts(T.rowc[:], T.qi[:], float(8 * r), A.add))
+    v(ts(T.odd[:], T.oi[:], 1.0, A.mult))
+    v(ts(T.even[:], T.oi[:], -1.0, A.mult, 1.0, A.add))
+    if edge:
+        for k in range(1, 5):
+            v(ts(T.kcol[:, k:k + 1], T.mi[:], 0.0, A.is_equal, float(-k if r == 0 else k), A.mult))
+    v(V.memset(T.w0[:], 0.0), "ms")
+    g.wait_ge(sem.sb, 1)
+    pat = [[-16, 9], [1000, 16]]
+    g.affine_select(T.sel[:], T.sel[:], pat, A.is_equal, 0.0, -15000, 1).then_inc(sem.sel1, 1)
+    g.wait_ge(sem.sel1, 1)
+    g.affine_select(T.sel[:], T.sel[:], pat, A.not_equal, 1.0, -15001, 1).then_inc(sem.sel2, 1)
+
+    V.wait_ge(sem.ldv, 32)
+    v(V.tensor_tensor(out=T.ci[:], in0=T.vxi[:], in1=T.xiota[:], op=A.add))
+    vs()
+    v(ts(T.dig[:, 0:4, :], T.vyi[:], T.rowc[:, 0:1], A.add), "dg")
+    v(ts(T.ci[:], T.ci[:], 127, A.bitwise_and))
+    vs()
+    v(V.tensor_copy(out=T.dig[:, 4:8, :], in_=T.ci[:]), "dg")
+
+    g.wait_ge(sem.dg, 2)
+    es = topo.engines(core, nb)
+    sent = 0
+    he = es[8:]
+    tr = [transfer(topo, core, nb, T.dnear[:], T.dig[:], he, sem.vn)]
+    sent += len(he)
+    if not edge:
+        rel = relays[(core, fb)]
+        tr.insert(0, transfer(topo, core, rel[0], T.rv[:], T.dig[:], es[:8], sem.rva))
+        sent += 8
+    g.remote_dma_fused(tr, local_sem=sem.sent)
+    g.wait_ge(sem.ldi, 32)
+    if not edge:
+        k = len(rel)
+        w, e = 1024 // k, len(es) // k
+        land = T.rp if k == 2 else T.rq
+        g.remote_dma_fused([transfer(topo, core, x, land[:], T.pic[:, 1024 + i * w:1024 + (i + 1) * w],
+                                     es[i * e:(i + 1) * e], sem.rpa) for i, x in enumerate(rel)], local_sem=sem.sent)
+        sent += len(es)
+    to = 0 if up else 2048
+    rid, pid = topo.addr(nb, core)
+    g.remote_dma(T.pic[:, to:to + 1024], T.pic[:, 1024:2048], sem.pnr, sem.sent, pid, rid, topo.mask(core, nb))
+    sent += len(es)
+
+    def spread(q1, q2, src, col, name):
+        q1.dma_start(out=T.w0[0:128:16, col:col + 1024], in_=src[:, 0:4, :]).then_inc(sem[name], 16)
+        q2.dma_start(out=T.w0[1:128:16, col:col + 1024], in_=src[:, 4:8, :]).then_inc(sem[name], 16)
+    for q in (SY, S):
+        q.wait_ge(sem.ms, 1)
+        q.wait_ge(sem.dg, 2)
+    spread(SY, S, T.dig, 1024, "rs_o")
+    ncol, fcol = (2048, 0) if up else (0, 2048)
+    SY.wait_ge(sem.vn, 8)
+    spread(SY, SY, T.dnear, ncol, "rs_n")
+    fe = 8
+    if not edge:
+        SY.wait_ge(sem.vf, fe)
+        spread(SY, SY, T.dfar, fcol, "rs_f")
+
+    def first_list(src, base, outs, name):
+        v(ts(T.t1[:], src[:, 0:4, :], 128.0, A.mult, float(-128 * (top + base)), A.add))
+        vs()
+        v(V.tensor_tensor(out=T.gg[:], in0=T.t1[:], in1=src[:, 4:8, :], op=A.add))
+        vs()
+        v(ts(T.blk[:, :, 0:16], T.gg[:], T.even[:, 0:1], A.mult))
+        v(ts(T.blk[:, :, 16:32], T.gg[:], T.odd[:, 0:1], A.mult))
+        vs()
+        for b in range(4):
+            v(V.transpose(out=T.tb[:, b, :], in_=T.blk[:, b, :]))
+        vs()
+        for b in range(4):
+            v(V.tensor_tensor(out=T.lf[:, b:64:4], in0=T.tb[:, b, 0:16], in1=T.tb[:, b, 16:32], op=A.add))
+        vs()
+        for c, m0, m1, add in outs:
+            v(ts(T.l0[:, c:c + m1 - m0], T.lf[:, m0:m1], float(add), A.add), name)
+        V.wait_ge(sem[name], len(outs))
+
+    def gather(out, win, lo, hi, lst, rows, o0, names):
+        a, b = 8 * rows[0], 8 * rows[1]
+        m = a + (b - a) // 4 * 2
+        d = 8 * o0
+        W = win[:, 128 * lo:128 * hi]
+        V.tensor_copy(out=out[:, 16 * (a - d):16 * (m - d)], in_=W.indirect(lst[:, a - d:m - d])).then_inc(sem[names[0]], 1)
+        S.activation(out=out[:, 16 * (m - d):16 * (b - d)], in_=W.indirect(lst[:, m - d:b - d]),
+                     func=F.Copy).then_inc(sem[names[1]], 1)
+
+    def pick(ps, win, rows, o0, name):
+        a, b = 128 * (rows[0] - o0), 128 * (rows[1] - o0)
+        k = (b - a) // 16
+        for q in range(16):
+            ins = TE.matmul(ps[:, 0:k], T.sel[:, 15 - q:143 - q], win[:, a + q:b:16], q == 0, q == 15)
+        ins.then_inc(sem[name], 1)
+        return k
+
+    def both(name, k):
+        V.wait_ge(sem[name], k)
+        S.wait_ge(sem[name], k)
+
+    if edge:
+        lo_n, lo_f = ((8, 24), (7, 16)) if up else ((0, 16), (8, 17))
+        fr0 = (8, 9) if up else (15, 16)
+        fr1 = (8, 11) if up else (13, 16)
+        fw1 = (6, 16) if up else (9, 18)
+        w2w = (4, 20)
+        pw = (8, 24) if up else (0, 16)
+    else:
+        lo_n, lo_f = ((8, 24), (0, 16)) if up else ((0, 16), (8, 24))
+        fr0 = (2, 9) if up else (15, 22)
+        fr1 = (4, 11) if up else (13, 20)
+        fw1 = (2, 16) if up else (9, 22)
+        w2w = (4, 20)
+        pw = (0, 24)
+    nr0 = (15, 22) if up else (2, 9)
+    nr1 = (11, 20) if up else (4, 13)
+    nw1 = (9, 22) if up else (2, 15)
+    halo = {True: (8, [(128, 0, 48, 0)]), False: (0, [(16, 16, 64, 0)])}
+    low_base = (lo_f if up else lo_n)[0]
+
+    first_list(T.dig, 8, [(72, 8, 64, 0), (64, 0, 8, 128 * (8 - low_base))], "lo")
+    V.wait_ge(sem.ms, 1)
+    V.wait_ge(sem.dg, 2)
+    S.wait_ge(sem.lo, 2)
+    both("rs_o", 32)
+    gather(T.w1, T.w0, 8, 16, T.l0, (9, 15), 0, ("g_e", "g_e"))
+    if edge:
+        a, b = (8, 7) if up else (15, 16)
+        v(ts(T.w0[:, 128 * b:128 * b + 128], T.w0[:, 128 * a:128 * a + 128], T.kcol[:, 1:2], A.add), "vir0")
+
+    V.wait_ge(sem.vn, 8)
+    first_list(T.dnear, halo[up][0], halo[up][1], "ln")
+    S.wait_ge(sem.ln, 1)
+    both("rs_n", 32)
+    gather(T.w1, T.w0, lo_n[0], lo_n[1], T.l0, nr0, 0, ("g_n", "g_n"))
+    TE.wait_ge(sem.sel2, 1)
+    TE.wait_ge(sem.g_e, 2)
+    TE.wait_ge(sem.g_n, 2)
+    kn = pick(T.pn, T.w1, nr1, 0, "t_n")
+
+    if not edge:
+        V.wait_ge(sem.vf, fe)
+        first_list(T.dfar, halo[not up][0], halo[not up][1], "lfar")
+        S.wait_ge(sem.lfar, 1)
+    V.wait_ge(sem.t_n, 1)
+    v(ts(T.l1[:, 8 * nr1[0]:8 * nr1[1]], T.pn[:, 0:kn], float(-128 * (top + nw1[0])), A.add), "c_n")
+    if edge:
+        both("vir0", 1)
+    else:
+        both("rs_f", 32)
+    gather(T.w1, T.w0, lo_f[0], lo_f[1], T.l0, fr0, 0, ("g_f", "g_f"))
+    both("c_n", 1)
+    gather(T.w2, T.w1, nw1[0], nw1[1], T.l1, nr1, 0, ("h_n", "h_n"))
+    TE.wait_ge(sem.g_f, 2)
+    kf = pick(T.pf, T.w1, fr1, 0, "t_f")
+
+    def beyond(win, ks, name, wait):
+        V.wait_ge(sem[wait], 2)
+        for k in ks:
+            a, b = (8, 8 - k) if up else (15, 15 + k)
+            v(ts(win[:, 128 * b:128 * b + 128], win[:, 128 * a:128 * a + 128], T.kcol[:, k:k + 1], A.add), name)
+        both(name, len(ks))
+
+    if edge:
+        beyond(T.w1, (1, 2), "vir1", "g_f")
+    V.wait_ge(sem.t_f, 1)
+    v(ts(T.l1[:, 8 * fr1[0]:8 * fr1[1]], T.pf[:, 0:kf], float(-128 * (top + fw1[0])), A.add), "c_f")
+    both("c_f", 1)
+    gather(T.w2, T.w1, fw1[0], min(fw1[1], 16) if up else fw1[1], T.l1, fr1, 0, ("h_f", "h_f"))
+
+    TE.wait_ge(sem.h_n, 2)
+    TE.wait_ge(sem.h_f, 2)
+    pick(T.p2, T.w2, (8, 16), 0, "t_2")
+    if edge:
+        V.wait_ge(sem.h_n, 2)
+        beyond(T.w2, (1, 2, 3, 4), "vir2", "h_f")
+    V.wait_ge(sem.t_2, 1)
+    v(ts(T.l2[:], T.p2[:, 0:64], float(-128 * (top + w2w[0])), A.add), "c_2")
+    both("c_2", 1)
+    gather(T.w3, T.w2, w2w[0], w2w[1], T.l2, (8, 16), 8, ("g_2", "g_2"))
+
+    TE.wait_ge(sem.g_2, 2)
+    pick(T.p3, T.w3, (8, 16), 8, "t_3")
+    V.wait_ge(sem.t_3, 1)
+    if edge:
+        v(ts(T.li[:], T.p3[:, 0:64], float(-128 * top), A.add))
+        vs()
+        v(ts(T.la[:], T.li[:], 127, A.bitwise_and))
+        v(ts(T.lb[:], T.li[:], 7, A.arith_shift_right))
+        vs()
+        v(ts(T.lb[:], T.lb[:], 8.0 if up else 15.0, A.max if up else A.min, -float(pw[0]), A.add))
+        vs()
+        v(ts(T.li[:], T.lb[:], 128.0, A.mult))
+        vs()
+        v(V.tensor_tensor(out=T.li[:], in0=T.li[:], in1=T.la[:], op=A.add))
+        vs()
+        v(V.tensor_copy(out=T.l3[:], in_=T.li[:]), "c_3")
+    else:
+        v(ts(T.l3[:], T.p3[:, 0:64], float(-128 * top), A.add), "c_3")
+    both("c_3", 1)
+    both("ldi", 32)
+    both("pnr", 16)
+    if not edge:
+        both("pfr", 8 * len(relays[(fb, core)]))
+    gather(T.yo, T.pic, pw[0], pw[1], T.l3, (8, 16), 8, ("g_3v", "g_3s"))
+    SY.wait_ge(sem.g_3v, 1)
+    SY.dma_start(out=T.y[:, 0:512], in_=T.yo[:, 0:512]).then_inc(sem.sty_a, 16)
+    S.wait_ge(sem.g_3s, 1)
+    S.dma_start(out=T.y[:, 512:1024], in_=T.yo[:, 512:1024]).then_inc(sem.sty_b, 16)
+    vs()
+    g.wait_ge(sem.sent, sent)
+    g.wait_ge(sem.sty_a, 16)
+    g.wait_ge(sem.sty_b, 16)
+
+
+def hand_on(g, core, T, topo, s, d, rel):
+    sem = T.sem
+    k, i = len(rel), rel.index(core)
+    w = 1024 // k
+    land = T.rp if k == 2 else T.rq
+    rid, pid = topo.addr(d, core)
+    es = topo.engines(core, d)
+    up = T.rank_of(d) > T.rank_of(s)
+    n = 0
+    if i == 0:
+        g.wait_ge(sem.rva, 8)
+        g.remote_dma(T.dfar[:], T.rv[:], sem.vf, sem.rsent, pid, rid, topo.mask(core, d))
+        n += len(es)
+    g.wait_ge(sem.rpa, len(topo.engines(s, core)) // k)
+    c = (0 if up else 2048) + i * w
+    g.remote_dma(T.pic[:, c:c + w], land[:], sem.pfr, sem.rsent, pid, rid, topo.mask(core, d))
+    g.wait_ge(sem.rsent, n + len(es))

@@ -2,28 +2,36 @@ from concourse.bass import DstId, RemoteDMATransfer
 from concourse.mybir import AluOpType as A, ActivationFunctionType as F
 
 BF, F32, I32, U16 = "bfloat16", "float32", "int32", "uint16"
+SIM_CORES = 256
+W_OUT, W_OVER = 320, 192
+DIG_ENGINES = 4
 SCRATCH = {
+    "v2i": ("sbuf", [128, 128], I32), "miota": ("sbuf", [128, 128], I32),
     "vyi": ("sbuf", [128, 4, 16], I32), "vxi": ("sbuf", [128, 4, 16], I32), "ci": ("sbuf", [128, 4, 16], I32),
-    "xiota": ("sbuf", [128, 4, 16], I32), "pidx": ("sbuf", [128, 1], I32), "qi": ("sbuf", [128, 1], I32),
-    "oi": ("sbuf", [128, 1], I32), "rowc": ("sbuf", [128, 1], F32), "odd": ("sbuf", [128, 1], F32),
-    "even": ("sbuf", [128, 1], F32), "mi": ("sbuf", [128, 1], I32), "kcol": ("sbuf", [128, 8], F32),
-    "dig": ("sbuf", [128, 8, 16], BF), "dnear": ("sbuf", [128, 8, 16], BF), "dfar": ("sbuf", [128, 8, 16], BF),
+    "xiota": ("sbuf", [128, 4, 16], I32), "pidx": ("sbuf", [128, 1], I32), "hi": ("sbuf", [128, 1], I32),
+    "oi": ("sbuf", [128, 1], I32), "pi": ("sbuf", [128, 1], I32), "mi": ("sbuf", [128, 1], I32),
+    "hrow": ("sbuf", [128, 1], F32), "h128": ("sbuf", [128, 1], F32),
+    "odd": ("sbuf", [128, 1], F32), "even": ("sbuf", [128, 1], F32), "kcol": ("sbuf", [128, 8], F32),
+    "dig": ("sbuf", [128, 128], BF), "dnear": ("sbuf", [128, 128], BF), "dfar": ("dram", [128, 128], BF),
     "t1": ("sbuf", [128, 4, 16], F32), "gg": ("sbuf", [128, 4, 16], F32),
+    "gnear": ("sbuf", [128, 4, 16], F32), "gfar": ("sbuf", [128, 4, 16], F32),
     "blk": ("sbuf", [128, 4, 32], F32), "tb": ("sbuf", [128, 4, 32], F32), "lf": ("sbuf", [128, 64], F32),
-    "l0": ("sbuf", [128, 192], U16), "l1": ("sbuf", [128, 192], U16), "l2": ("sbuf", [128, 64], U16),
-    "l3": ("sbuf", [128, 64], U16),
+    "l0": ("sbuf", [128, 192], U16), "l1": ("sbuf", [128, 192], U16), "l2": ("sbuf", [128, 192], U16),
+    "l2e": ("sbuf", [128, 64], U16), "l3": ("sbuf", [128, 64], U16),
     "li": ("sbuf", [128, 64], I32), "la": ("sbuf", [128, 64], I32), "lb": ("sbuf", [128, 64], I32),
     "w0": ("sbuf", [128, 3072], BF), "w1": ("sbuf", [128, 3072], BF), "w2": ("sbuf", [128, 3072], BF),
-    "w3": ("sbuf", [128, 1024], BF), "pic": ("sbuf", [128, 3072], BF), "yo": ("sbuf", [128, 1024], BF),
+    "jb": ("sbuf", [128, 3072], BF), "pic": ("sbuf", [128, 3072], BF), "yo": ("sbuf", [128, 1024], BF),
     "sel": ("sbuf", [128, 144], BF),
-    "rv": ("sbuf", [128, 8, 16], BF), "rp": ("sbuf", [128, 512], BF), "rq": ("sbuf", [128, 256], BF),
-    "pn": ("psum", [128, 512], F32), "pf": ("psum", [128, 512], F32),
+    "rv": ("dram", [128, 128], BF), "rg": ("sbuf", [128, 4, 16], F32),
+    "rp": ("sbuf", [128, W_OUT], BF), "rq": ("sbuf", [128, W_OVER], BF),
+    "bp": ("psum", [128, 512], F32), "pn": ("psum", [128, 512], F32), "pf": ("psum", [128, 512], F32),
     "p2": ("psum", [128, 512], F32), "p3": ("psum", [128, 512], F32),
 }
-SEMAPHORES = ["vc", "gi", "ldv", "ldi", "ms", "sb", "sel1", "sel2", "dg", "rs_o", "rs_n", "rs_f", "lo", "ln", "lfar",
-              "g_e", "g_n", "g_f", "h_n", "h_f", "g_2", "g_3v", "g_3s", "t_n", "t_f", "t_2", "t_3",
+SEMAPHORES = ["vc", "gi", "ldc", "ldv", "ldi", "ldj", "ms", "msh", "msj", "sb", "sel1", "sel2", "dg", "gd",
+              "rs_o", "rs_n", "rs_f", "lo", "ln", "lfar",
+              "g_e", "g_n", "g_f", "g_f2", "h_n", "h_f", "g_2", "g_j", "g_3a", "g_3b", "t_n", "t_f", "t_2", "t_3",
               "c_n", "c_f", "c_2", "c_3", "vir0", "vir1", "vir2",
-              "vn", "vf", "pnr", "pfr", "sent", "sty_a", "sty_b", "rva", "rpa", "rsent"]
+              "vn", "vf", "gvn", "gvf", "pnr", "pfr", "sent", "sty_a", "sty_b", "rva", "rga", "rpa", "rsent"]
 
 
 def plan(T, topo):
@@ -35,16 +43,17 @@ def plan(T, topo):
         else:
             far[a], far[b] = b, a
             flows += [(a, b), (b, a)]
-    relays = {}
+    out, over, used = {}, {}, set()
     for s, d in flows:
-        own = [f for f in flows if f[0] in topo.cores_of(s)]
-        k = own.index((s, d))
-        c = [x for x in topo.cores_of(s) if T.rank_of(x) is None and topo.may_write(x, d)]
-        if len(own) > 1:
-            by = [[x for x in c if topo.die(x) == e] for e in (0, 1)]
-            c = [y[k] for y in by]
-        relays[(s, d)] = sorted(c, key=lambda x: (topo.die(x) != topo.die(s), x))
-    return near, far, relays
+        for way, c in ((out, topo.cores_of(s)), (over, [x for x in range(SIM_CORES) if topo.mates(x, d)])):
+            pair = []
+            for e in (topo.die(s), 1 - topo.die(s)):
+                x = [x for x in c if T.rank_of(x) is None and x not in used and topo.die(x) == e
+                     and topo.may_write(x, d) and topo.may_write(s, x)][0]
+                used.add(x)
+                pair.append(x)
+            way[(s, d)] = pair
+    return near, far, out, over
 
 
 def bits(engines):
@@ -60,20 +69,31 @@ def transfer(topo, src, dst, out, in_, engines, sem):
                              src=in_, dst=out)
 
 
+def columns(way, i):
+    a = i * W_OVER if way == "over" else 2 * W_OVER + i * W_OUT
+    return a, a + (W_OVER if way == "over" else W_OUT)
+
+
+def split(topo, a, near, b):
+    leave = topo.engines(a, b)
+    return leave, [e for e in topo.engines(a, near) if e not in leave]
+
+
 def rank_program(g, core, T, topo):
-    near, far, relays = plan(T, topo)
+    near, far, out, over = plan(T, topo)
     sem = T.sem
     if T.rank_of(core) is None:
-        for (s, d), rel in relays.items():
-            if core in rel:
-                hand_on(g, core, T, topo, s, d, rel)
+        for name, way in (("out", out), ("over", over)):
+            for (s, d), rel in way.items():
+                if core in rel:
+                    hand_on(g, core, T, topo, s, d, name, rel.index(core), near[s])
         return
-    r, n = T.rank_of(core), len(T.cores)
+    r = T.rank_of(core)
     nb, fb = near[core], far.get(core)
     up = T.rank_of(nb) > r
     edge = fb is None
     V, S, TE, SY = g.vector, g.scalar, g.tensor, g.sync
-    top = 8 * r - 8
+    top = 8 * r
     cnt = [0, 0]
 
     def v(ins, name=None):
@@ -93,87 +113,116 @@ def rank_program(g, core, T, topo):
             return V.tensor_scalar(out=out, in0=in0, scalar1=s1, scalar2=None, op0=op0)
         return V.tensor_scalar(out=out, in0=in0, scalar1=s1, scalar2=s2, op0=op0, op1=op1)
 
+    cut = 2 * W_OVER
+    SY.dma_start(out=T.v2i[0:64, :], in_=T.vy[:]).then_inc(sem.ldc, 16)
+    S.dma_start(out=T.v2i[64:128, :], in_=T.vx[:]).then_inc(sem.ldc, 16)
     SY.dma_start(out=T.vyi[:], in_=T.vy[:]).then_inc(sem.ldv, 16)
     S.dma_start(out=T.vxi[:], in_=T.vx[:]).then_inc(sem.ldv, 16)
-    SY.dma_start(out=T.pic[:, 1024:1536], in_=T.img[:, 0:512]).then_inc(sem.ldi, 16)
-    S.dma_start(out=T.pic[:, 1536:2048], in_=T.img[:, 512:1024]).then_inc(sem.ldi, 16)
+    SY.dma_start(out=T.pic[:, 1024:1024 + cut], in_=T.img[:, 0:cut]).then_inc(sem.ldi, 16)
+    S.dma_start(out=T.pic[:, 1024 + cut:2048], in_=T.img[:, cut:1024]).then_inc(sem.ldj, 16)
 
     g.iota(out=T.pidx[:], pattern=[[1, 1]], base=0, channel_multiplier=1).then_inc(sem.gi, 1)
+    g.iota(out=T.miota[:], pattern=[[1, 128]], base=0, channel_multiplier=0).then_inc(sem.gi, 1)
     g.iota(out=T.xiota[:], pattern=[[16, 4], [1, 16]], base=0, channel_multiplier=64).then_inc(sem.gi, 1)
     v(V.memset(T.sel[:], 128.0), "sb")
-    V.wait_ge(sem.gi, 2)
-    v(ts(T.qi[:], T.pidx[:], 15, A.bitwise_and, 1, A.arith_shift_right))
+    v(V.memset(T.jb[:, 0:512], 0.0), "msj")
+    v(V.memset(T.w0[:, 1024:2048], 0.0), "ms")
+    S.wait_ge(sem.msj, 1)
+    for c in (0, 512, 2048, 2560):
+        S.activation(out=T.w0[:, c:c + 512], in_=T.jb[:, 0:512], func=F.Copy).then_inc(sem.msh, 1)
+    V.wait_ge(sem.gi, 3)
+    v(ts(T.pi[:], T.pidx[:], 7, A.bitwise_and))
+    v(ts(T.hi[:], T.pidx[:], 1, A.arith_shift_right, 7, A.bitwise_and))
     v(ts(T.oi[:], T.pidx[:], 4, A.arith_shift_right, 1, A.bitwise_and))
     if edge:
         v(ts(T.mi[:], T.pidx[:], 15, A.bitwise_and))
+    v(V.tensor_copy(out=T.bp[64:128, 0:128], in_=T.miota[64:128, :]))
     vs()
-    v(ts(T.rowc[:], T.qi[:], float(8 * r), A.add))
+    v(ts(T.hrow[:], T.pi[:], float(8 * r + 8), A.add))
+    v(ts(T.h128[:], T.hi[:], 128.0, A.mult, float(128 * (8 * r + 8)), A.add))
     v(ts(T.odd[:], T.oi[:], 1.0, A.mult))
     v(ts(T.even[:], T.oi[:], -1.0, A.mult, 1.0, A.add))
-    if edge:
-        for k in range(1, 5):
-            v(ts(T.kcol[:, k:k + 1], T.mi[:], 0.0, A.is_equal, float(-k if r == 0 else k), A.mult))
-    v(V.memset(T.w0[:], 0.0), "ms")
+    vs()
     g.wait_ge(sem.sb, 1)
     pat = [[-16, 9], [1000, 16]]
     g.affine_select(T.sel[:], T.sel[:], pat, A.is_equal, 0.0, -15000, 1).then_inc(sem.sel1, 1)
     g.wait_ge(sem.sel1, 1)
     g.affine_select(T.sel[:], T.sel[:], pat, A.not_equal, 1.0, -15001, 1).then_inc(sem.sel2, 1)
 
+    V.wait_ge(sem.ldc, 32)
+    v(V.tensor_tensor(out=T.v2i[64:128, :], in0=T.v2i[64:128, :], in1=T.bp[64:128, 0:128], op=A.add))
+    v(ts(T.dig[0:64, :], T.v2i[0:64, :], T.hrow[0:64, 0:1], A.add), "dg")
+    vs()
+    v(ts(T.v2i[64:128, :], T.v2i[64:128, :], 127, A.bitwise_and))
+    vs()
+    v(V.tensor_copy(out=T.dig[64:128, :], in_=T.v2i[64:128, :]), "dg")
     V.wait_ge(sem.ldv, 32)
     v(V.tensor_tensor(out=T.ci[:], in0=T.vxi[:], in1=T.xiota[:], op=A.add))
+    v(ts(T.t1[:], T.vyi[:], 128.0, A.mult, T.h128[:, 0:1], A.add))
     vs()
-    v(ts(T.dig[:, 0:4, :], T.vyi[:], T.rowc[:, 0:1], A.add), "dg")
     v(ts(T.ci[:], T.ci[:], 127, A.bitwise_and))
     vs()
-    v(V.tensor_copy(out=T.dig[:, 4:8, :], in_=T.ci[:]), "dg")
+    v(V.tensor_tensor(out=T.gg[:], in0=T.t1[:], in1=T.ci[:], op=A.add), "gd")
+    if edge:
+        for k in range(1, 5):
+            v(ts(T.kcol[:, k:k + 1], T.mi[:], 0.0, A.is_equal, float(-k if r == 0 else k), A.mult))
 
-    g.wait_ge(sem.dg, 2)
     es = topo.engines(core, nb)
-    sent = 0
-    he = es[8:]
-    tr = [transfer(topo, core, nb, T.dnear[:], T.dig[:], he, sem.vn)]
-    sent += len(he)
+    ref = core if not edge else nb
+    leave, stay = split(topo, ref, near[ref], over[(ref, far[ref])][0])
+    sent = [0]
+
+    def send(dst, to, src, engines, s):
+        rid, pid = topo.addr(dst, core)
+        g.remote_dma(to, src, s, sem.sent, pid, rid, bits(engines))
+        sent[0] += len(engines)
+
+    def image(dst, to, a, b, engines, s):
+        send(dst, to, T.pic[:, 1024 + a:1024 + b], engines, s)
+    g.wait_ge(sem.dg, 2)
     if not edge:
-        rel = relays[(core, fb)]
-        tr.insert(0, transfer(topo, core, rel[0], T.rv[:], T.dig[:], es[:8], sem.rva))
-        sent += 8
+        send(out[(core, fb)][0], T.rv[:], T.dig[:], leave, sem.rva)
+    send(nb, T.dnear[:], T.dig[:], stay, sem.vn)
+    g.wait_ge(sem.gd, 1)
+    tr = [transfer(topo, core, nb, T.gnear[:], T.gg[:], stay, sem.gvn)]
+    if not edge:
+        tr.insert(0, transfer(topo, core, out[(core, fb)][0], T.rg[:], T.gg[:], leave, sem.rga))
     g.remote_dma_fused(tr, local_sem=sem.sent)
-    g.wait_ge(sem.ldi, 32)
-    if not edge:
-        k = len(rel)
-        w, e = 1024 // k, len(es) // k
-        land = T.rp if k == 2 else T.rq
-        g.remote_dma_fused([transfer(topo, core, x, land[:], T.pic[:, 1024 + i * w:1024 + (i + 1) * w],
-                                     es[i * e:(i + 1) * e], sem.rpa) for i, x in enumerate(rel)], local_sem=sem.sent)
-        sent += len(es)
+    sent[0] += len(tr) * len(stay)
     to = 0 if up else 2048
-    rid, pid = topo.addr(nb, core)
-    g.remote_dma(T.pic[:, to:to + 1024], T.pic[:, 1024:2048], sem.pnr, sem.sent, pid, rid, topo.mask(core, nb))
-    sent += len(es)
+    g.wait_ge(sem.ldi, 16)
+    if edge:
+        g.wait_ge(sem.ldj, 16)
+        image(nb, T.pic[:, to:to + 1024], 0, 1024, es, sem.pnr)
+    else:
+        ro, rw = out[(core, fb)], over[(core, fb)]
+        image(rw[0], T.rq[:], *columns("over", 0), leave, sem.rpa)
+        g.wait_ge(sem.ldj, 16)
+        image(ro[0], T.rp[:], *columns("out", 0), stay, sem.rpa)
+        image(rw[1], T.rq[:], *columns("over", 1), leave, sem.rpa)
+        image(ro[1], T.rp[:], *columns("out", 1), stay, sem.rpa)
+        g.wait_ge(sem.rs_n, 32)
+        image(nb, T.pic[:, to:to + cut], 0, cut, stay, sem.pnr)
+    pn_inc = len(es) if far.get(nb) is None else (1 + len(out[(nb, far[nb])])) * len(stay)
 
     def spread(q1, q2, src, col, name):
-        q1.dma_start(out=T.w0[0:128:16, col:col + 1024], in_=src[:, 0:4, :]).then_inc(sem[name], 16)
-        q2.dma_start(out=T.w0[1:128:16, col:col + 1024], in_=src[:, 4:8, :]).then_inc(sem[name], 16)
+        q1.dma_start(out=T.w0[0:128:16, col:col + 1024], in_=src[0:64, :]).then_inc(sem[name], 16)
+        q2.dma_start(out=T.w0[1:128:16, col:col + 1024], in_=src[64:128, :]).then_inc(sem[name], 16)
     for q in (SY, S):
         q.wait_ge(sem.ms, 1)
         q.wait_ge(sem.dg, 2)
     spread(SY, S, T.dig, 1024, "rs_o")
     ncol, fcol = (2048, 0) if up else (0, 2048)
-    SY.wait_ge(sem.vn, 8)
+    SY.wait_ge(sem.msh, 4)
+    SY.wait_ge(sem.vn, len(stay))
     spread(SY, SY, T.dnear, ncol, "rs_n")
-    fe = 8
     if not edge:
-        SY.wait_ge(sem.vf, fe)
+        SY.wait_ge(sem.vf, DIG_ENGINES)
         spread(SY, SY, T.dfar, fcol, "rs_f")
 
     def first_list(src, base, outs, name):
-        v(ts(T.t1[:], src[:, 0:4, :], 128.0, A.mult, float(-128 * (top + base)), A.add))
-        vs()
-        v(V.tensor_tensor(out=T.gg[:], in0=T.t1[:], in1=src[:, 4:8, :], op=A.add))
-        vs()
-        v(ts(T.blk[:, :, 0:16], T.gg[:], T.even[:, 0:1], A.mult))
-        v(ts(T.blk[:, :, 16:32], T.gg[:], T.odd[:, 0:1], A.mult))
+        v(ts(T.blk[:, :, 0:16], src[:], T.even[:, 0:1], A.mult))
+        v(ts(T.blk[:, :, 16:32], src[:], T.odd[:, 0:1], A.mult))
         vs()
         for b in range(4):
             v(V.transpose(out=T.tb[:, b, :], in_=T.blk[:, b, :]))
@@ -182,20 +231,25 @@ def rank_program(g, core, T, topo):
             v(V.tensor_tensor(out=T.lf[:, b:64:4], in0=T.tb[:, b, 0:16], in1=T.tb[:, b, 16:32], op=A.add))
         vs()
         for c, m0, m1, add in outs:
-            v(ts(T.l0[:, c:c + m1 - m0], T.lf[:, m0:m1], float(add), A.add), name)
+            v(ts(T.l0[:, c:c + m1 - m0], T.lf[:, m0:m1], float(add - 128 * (top + base)), A.add), name)
         V.wait_ge(sem[name], len(outs))
 
-    def gather(out, win, lo, hi, lst, rows, o0, names):
+    def part(eng, out, W, lst, a, b, d, f, name):
+        o, i = out[:, 16 * (a - d):16 * (b - d)], W.indirect(lst[:, a - f:b - f])
+        if eng is V:
+            V.tensor_copy(out=o, in_=i).then_inc(sem[name], 1)
+        else:
+            S.activation(out=o, in_=i, func=F.Copy).then_inc(sem[name], 1)
+
+    def gather(out, win, lo, hi, lst, rows, o0, name, l0=None):
         a, b = 8 * rows[0], 8 * rows[1]
         m = a + (b - a) // 4 * 2
-        d = 8 * o0
-        W = win[:, 128 * lo:128 * hi]
-        V.tensor_copy(out=out[:, 16 * (a - d):16 * (m - d)], in_=W.indirect(lst[:, a - d:m - d])).then_inc(sem[names[0]], 1)
-        S.activation(out=out[:, 16 * (m - d):16 * (b - d)], in_=W.indirect(lst[:, m - d:b - d]),
-                     func=F.Copy).then_inc(sem[names[1]], 1)
+        d, f = 8 * o0, 8 * (o0 if l0 is None else l0)
+        part(V, out, win[:, 128 * lo:128 * hi], lst, a, m, d, f, name)
+        part(S, out, win[:, 128 * lo:128 * hi], lst, m, b, d, f, name)
 
-    def pick(ps, win, rows, o0, name):
-        a, b = 128 * (rows[0] - o0), 128 * (rows[1] - o0)
+    def pick(ps, win, rows, name):
+        a, b = 128 * rows[0], 128 * rows[1]
         k = (b - a) // 16
         for q in range(16):
             ins = TE.matmul(ps[:, 0:k], T.sel[:, 15 - q:143 - q], win[:, a + q:b:16], q == 0, q == 15)
@@ -208,59 +262,61 @@ def rank_program(g, core, T, topo):
 
     if edge:
         lo_n, lo_f = ((8, 24), (7, 16)) if up else ((0, 16), (8, 17))
-        fr0 = (8, 9) if up else (15, 16)
+        fr0, fr0b = ((8, 9) if up else (15, 16)), None
         fr1 = (8, 11) if up else (13, 16)
         fw1 = (6, 16) if up else (9, 18)
-        w2w = (4, 20)
-        pw = (8, 24) if up else (0, 16)
     else:
         lo_n, lo_f = ((8, 24), (0, 16)) if up else ((0, 16), (8, 24))
-        fr0 = (2, 9) if up else (15, 22)
+        fr0, fr0b = ((4, 9), (2, 4)) if up else ((15, 20), (20, 22))
         fr1 = (4, 11) if up else (13, 20)
         fw1 = (2, 16) if up else (9, 22)
-        w2w = (4, 20)
-        pw = (0, 24)
     nr0 = (15, 22) if up else (2, 9)
     nr1 = (11, 20) if up else (4, 13)
     nw1 = (9, 22) if up else (2, 15)
     halo = {True: (8, [(128, 0, 48, 0)]), False: (0, [(16, 16, 64, 0)])}
     low_base = (lo_f if up else lo_n)[0]
 
-    first_list(T.dig, 8, [(72, 8, 64, 0), (64, 0, 8, 128 * (8 - low_base))], "lo")
+    V.wait_ge(sem.gd, 1)
+    first_list(T.gg, 8, [(72, 8, 64, 0), (64, 0, 8, 128 * (8 - low_base))], "lo")
     V.wait_ge(sem.ms, 1)
-    V.wait_ge(sem.dg, 2)
+    both("msh", 4)
     S.wait_ge(sem.lo, 2)
     both("rs_o", 32)
-    gather(T.w1, T.w0, 8, 16, T.l0, (9, 15), 0, ("g_e", "g_e"))
+    gather(T.w1, T.w0, 8, 16, T.l0, (9, 15), 0, "g_e")
     if edge:
         a, b = (8, 7) if up else (15, 16)
         v(ts(T.w0[:, 128 * b:128 * b + 128], T.w0[:, 128 * a:128 * a + 128], T.kcol[:, 1:2], A.add), "vir0")
 
-    V.wait_ge(sem.vn, 8)
-    first_list(T.dnear, halo[up][0], halo[up][1], "ln")
+    V.wait_ge(sem.gvn, len(stay))
+    first_list(T.gnear, halo[up][0], halo[up][1], "ln")
     S.wait_ge(sem.ln, 1)
     both("rs_n", 32)
-    gather(T.w1, T.w0, lo_n[0], lo_n[1], T.l0, nr0, 0, ("g_n", "g_n"))
+    gather(T.w1, T.w0, lo_n[0], lo_n[1], T.l0, nr0, 0, "g_n")
     TE.wait_ge(sem.sel2, 1)
     TE.wait_ge(sem.g_e, 2)
     TE.wait_ge(sem.g_n, 2)
-    kn = pick(T.pn, T.w1, nr1, 0, "t_n")
-
-    if not edge:
-        V.wait_ge(sem.vf, fe)
-        first_list(T.dfar, halo[not up][0], halo[not up][1], "lfar")
-        S.wait_ge(sem.lfar, 1)
+    kn = pick(T.pn, T.w1, nr1, "t_n")
     V.wait_ge(sem.t_n, 1)
     v(ts(T.l1[:, 8 * nr1[0]:8 * nr1[1]], T.pn[:, 0:kn], float(-128 * (top + nw1[0])), A.add), "c_n")
-    if edge:
-        both("vir0", 1)
-    else:
+    S.wait_ge(sem.c_n, 1)
+    n0, wn = 8 * nr1[0], T.w1[:, 128 * nw1[0]:128 * nw1[1]]
+    part(S, T.w2, wn, T.l1, n0, n0 + 24, 0, 0, "h_n")
+
+    if not edge:
+        V.wait_ge(sem.gvf, len(topo.engines(out[(fb, core)][0], core)))
+        first_list(T.gfar, halo[not up][0], halo[not up][1], "lfar")
+        S.wait_ge(sem.lfar, 1)
         both("rs_f", 32)
-    gather(T.w1, T.w0, lo_f[0], lo_f[1], T.l0, fr0, 0, ("g_f", "g_f"))
-    both("c_n", 1)
-    gather(T.w2, T.w1, nw1[0], nw1[1], T.l1, nr1, 0, ("h_n", "h_n"))
+    else:
+        both("vir0", 1)
+    gather(T.w1, T.w0, lo_f[0], lo_f[1], T.l0, fr0, 0, "g_f")
     TE.wait_ge(sem.g_f, 2)
-    kf = pick(T.pf, T.w1, fr1, 0, "t_f")
+    kf = pick(T.pf, T.w1, fr1, "t_f")
+    if not edge:
+        gather(T.w1, T.w0, lo_f[0], lo_f[1], T.l0, fr0b, 0, "g_f2")
+    V.wait_ge(sem.c_n, 1)
+    part(V, T.w2, wn, T.l1, n0 + 24, n0 + 48, 0, 0, "h_n")
+    part(S, T.w2, wn, T.l1, n0 + 48, n0 + 72, 0, 0, "h_n")
 
     def beyond(win, ks, name, wait):
         V.wait_ge(sem[wait], 2)
@@ -274,67 +330,88 @@ def rank_program(g, core, T, topo):
     V.wait_ge(sem.t_f, 1)
     v(ts(T.l1[:, 8 * fr1[0]:8 * fr1[1]], T.pf[:, 0:kf], float(-128 * (top + fw1[0])), A.add), "c_f")
     both("c_f", 1)
-    gather(T.w2, T.w1, fw1[0], min(fw1[1], 16) if up else fw1[1], T.l1, fr1, 0, ("h_f", "h_f"))
+    if not edge:
+        both("g_f2", 2)
+    gather(T.w2, T.w1, fw1[0], fw1[1], T.l1, fr1, 0, "h_f")
 
-    TE.wait_ge(sem.h_n, 2)
+    er, fr = ((12, 20), (4, 12)) if up else ((4, 12), (12, 20))
+    ew = (8, 24) if up else (0, 16)
+    TE.wait_ge(sem.h_n, 3)
+    pick(T.p2, T.w2, er, "t_2")
     TE.wait_ge(sem.h_f, 2)
-    pick(T.p2, T.w2, (8, 16), 0, "t_2")
     if edge:
-        V.wait_ge(sem.h_n, 2)
+        V.wait_ge(sem.h_n, 3)
         beyond(T.w2, (1, 2, 3, 4), "vir2", "h_f")
+        TE.wait_ge(sem.vir2, 4)
+    pick(T.p3, T.w2, fr, "t_3")
     V.wait_ge(sem.t_2, 1)
-    v(ts(T.l2[:], T.p2[:, 0:64], float(-128 * (top + w2w[0])), A.add), "c_2")
-    both("c_2", 1)
-    gather(T.w3, T.w2, w2w[0], w2w[1], T.l2, (8, 16), 8, ("g_2", "g_2"))
-
-    TE.wait_ge(sem.g_2, 2)
-    pick(T.p3, T.w3, (8, 16), 8, "t_3")
+    v(ts(T.l2e[:], T.p2[:, 0:64], float(-128 * (top + ew[0])), A.add), "c_2")
+    v(ts(T.l2[:, 8 * er[0]:8 * er[1]], T.p2[:, 0:64], float(-128 * top), A.add), "c_2")
+    both("c_2", 2)
+    both("ldi", 16)
+    both("ldj", 16)
+    both("pnr", pn_inc)
+    gather(T.jb, T.pic, ew[0], ew[1], T.l2e, er, 0, "g_2", er[0])
     V.wait_ge(sem.t_3, 1)
+    v(ts(T.l2[:, 8 * fr[0]:8 * fr[1]], T.p3[:, 0:64], float(-128 * top), A.add), "c_3")
     if edge:
         v(ts(T.li[:], T.p3[:, 0:64], float(-128 * top), A.add))
         vs()
         v(ts(T.la[:], T.li[:], 127, A.bitwise_and))
         v(ts(T.lb[:], T.li[:], 7, A.arith_shift_right))
         vs()
-        v(ts(T.lb[:], T.lb[:], 8.0 if up else 15.0, A.max if up else A.min, -float(pw[0]), A.add))
+        v(ts(T.lb[:], T.lb[:], 8.0 if up else 15.0, A.max if up else A.min, -float(ew[0]), A.add))
         vs()
         v(ts(T.li[:], T.lb[:], 128.0, A.mult))
         vs()
         v(V.tensor_tensor(out=T.li[:], in0=T.li[:], in1=T.la[:], op=A.add))
         vs()
         v(V.tensor_copy(out=T.l3[:], in_=T.li[:]), "c_3")
+    both("c_3", 2 if edge else 1)
+    if edge:
+        gather(T.jb, T.pic, ew[0], ew[1], T.l3, fr, 0, "g_j", fr[0])
     else:
-        v(ts(T.l3[:], T.p3[:, 0:64], float(-128 * top), A.add), "c_3")
-    both("c_3", 1)
-    both("ldi", 32)
-    both("pnr", 16)
-    if not edge:
-        both("pfr", 8 * len(relays[(fb, core)]))
-    gather(T.yo, T.pic, pw[0], pw[1], T.l3, (8, 16), 8, ("g_3v", "g_3s"))
-    SY.wait_ge(sem.g_3v, 1)
+        both("pfr", sum(len(topo.engines(x, core)) for x in out[(fb, core)] + over[(fb, core)]))
+        gather(T.jb, T.pic, 0, 24, T.l2, fr, 0, "g_j")
+    both("g_2", 2)
+    both("g_j", 2)
+    both("msj", 1)
+    gather(T.yo, T.jb, 0, 20, T.l2, (8, 12), 8, "g_3a", 0)
+    gather(T.yo, T.jb, 0, 20, T.l2, (12, 16), 8, "g_3b", 0)
+    SY.wait_ge(sem.g_3a, 2)
     SY.dma_start(out=T.y[:, 0:512], in_=T.yo[:, 0:512]).then_inc(sem.sty_a, 16)
-    S.wait_ge(sem.g_3s, 1)
+    S.wait_ge(sem.g_3b, 2)
     S.dma_start(out=T.y[:, 512:1024], in_=T.yo[:, 512:1024]).then_inc(sem.sty_b, 16)
     vs()
-    g.wait_ge(sem.sent, sent)
+    g.wait_ge(sem.sent, sent[0])
     g.wait_ge(sem.sty_a, 16)
     g.wait_ge(sem.sty_b, 16)
 
 
-def hand_on(g, core, T, topo, s, d, rel):
+def hand_on(g, core, T, topo, s, d, way, i, nb):
     sem = T.sem
-    k, i = len(rel), rel.index(core)
-    w = 1024 // k
-    land = T.rp if k == 2 else T.rq
     rid, pid = topo.addr(d, core)
-    es = topo.engines(core, d)
-    up = T.rank_of(d) > T.rank_of(s)
-    n = 0
+    m, ne = topo.mask(core, d), len(topo.engines(core, d))
+    es = topo.engines(s, core)
+    a, b = columns(way, i)
+    o = 0 if T.rank_of(d) > T.rank_of(s) else 2048
+    if way == "over":
+        g.wait_ge(sem.rpa, len(es))
+        g.remote_dma(T.pic[:, o + a:o + b], T.rq[:], sem.pfr, sem.rsent, pid, rid, m)
+        g.wait_ge(sem.rsent, ne)
+        return
+    leave, stay = split(topo, core, nb, d)
+    n = ne + len(stay)
+    half = len(es) // 2
     if i == 0:
-        g.wait_ge(sem.rva, 8)
-        g.remote_dma(T.dfar[:], T.rv[:], sem.vf, sem.rsent, pid, rid, topo.mask(core, d))
-        n += len(es)
-    g.wait_ge(sem.rpa, len(topo.engines(s, core)) // k)
-    c = (0 if up else 2048) + i * w
-    g.remote_dma(T.pic[:, c:c + w], land[:], sem.pfr, sem.rsent, pid, rid, topo.mask(core, d))
-    g.wait_ge(sem.rsent, n + len(es))
+        g.wait_ge(sem.rva, half)
+        g.remote_dma(T.dfar[:], T.rv[:], sem.vf, sem.rsent, pid, rid, bits(leave[:DIG_ENGINES]))
+        g.wait_ge(sem.rga, half)
+        g.remote_dma(T.gfar[:], T.rg[:], sem.gvf, sem.rsent, pid, rid, m)
+        n += DIG_ENGINES + ne
+    g.wait_ge(sem.rpa, half)
+    g.remote_dma(T.pic[:, o + a:o + b], T.rp[:], sem.pfr, sem.rsent, pid, rid, m)
+    o = 0 if T.rank_of(nb) > T.rank_of(s) else 2048
+    rid, pid = topo.addr(nb, core)
+    g.remote_dma(T.pic[:, o + a:o + b], T.rp[:], sem.pnr, sem.rsent, pid, rid, bits(stay))
+    g.wait_ge(sem.rsent, n)

@@ -6,32 +6,30 @@ SIM_CORES = 256
 W_OUT, W_OVER = 320, 192
 DIG_ENGINES = 4
 SCRATCH = {
-    "v2i": ("sbuf", [128, 128], I32), "miota": ("sbuf", [128, 128], I32),
     "vyi": ("sbuf", [128, 4, 16], I32), "vxi": ("sbuf", [128, 4, 16], I32), "ci": ("sbuf", [128, 4, 16], I32),
     "xiota": ("sbuf", [128, 4, 16], I32), "pidx": ("sbuf", [128, 1], I32), "hi": ("sbuf", [128, 1], I32),
-    "oi": ("sbuf", [128, 1], I32), "pi": ("sbuf", [128, 1], I32), "mi": ("sbuf", [128, 1], I32),
+    "oi": ("sbuf", [128, 1], I32), "mi": ("sbuf", [128, 1], I32),
     "hrow": ("sbuf", [128, 1], F32), "h128": ("sbuf", [128, 1], F32),
     "odd": ("sbuf", [128, 1], F32), "even": ("sbuf", [128, 1], F32), "kcol": ("sbuf", [128, 8], F32),
-    "dig": ("sbuf", [128, 128], BF), "dnear": ("sbuf", [128, 128], BF), "dfar": ("dram", [128, 128], BF),
-    "t1": ("sbuf", [128, 4, 16], F32), "gg": ("sbuf", [128, 4, 16], F32),
-    "gnear": ("sbuf", [128, 4, 16], F32), "gfar": ("sbuf", [128, 4, 16], F32),
-    "blk": ("sbuf", [128, 4, 32], F32), "tb": ("sbuf", [128, 4, 32], F32), "lf": ("sbuf", [128, 64], F32),
+    "dig": ("sbuf", [128, 8, 16], BF), "dnear": ("sbuf", [128, 8, 16], BF),
+    "dfr": ("dram", [128, 4, 16], BF), "dfc": ("dram", [128, 4, 16], BF),
+    "gg": ("sbuf", [128, 4, 16], F32), "blk": ("sbuf", [128, 4, 32], F32), "tb": ("sbuf", [128, 128], F32),
+    "lf": ("sbuf", [128, 64], F32), "lsn": ("sbuf", [128, 64], U16), "lsf": ("sbuf", [128, 64], U16),
     "l0": ("sbuf", [128, 192], U16), "l1": ("sbuf", [128, 192], U16), "l2": ("sbuf", [128, 192], U16),
-    "l2e": ("sbuf", [128, 64], U16), "l3": ("sbuf", [128, 64], U16),
-    "li": ("sbuf", [128, 64], I32), "la": ("sbuf", [128, 64], I32), "lb": ("sbuf", [128, 64], I32),
+    "l2e": ("sbuf", [128, 64], U16),
     "w0": ("sbuf", [128, 3072], BF), "w1": ("sbuf", [128, 3072], BF), "w2": ("sbuf", [128, 3072], BF),
     "jb": ("sbuf", [128, 3072], BF), "pic": ("sbuf", [128, 3072], BF), "yo": ("sbuf", [128, 1024], BF),
     "sel": ("sbuf", [128, 144], BF),
-    "rv": ("dram", [128, 128], BF), "rg": ("sbuf", [128, 4, 16], F32),
+    "rvr": ("dram", [128, 4, 16], BF), "rvc": ("dram", [128, 4, 16], BF), "rg": ("sbuf", [128, 64], U16),
     "rp": ("sbuf", [128, W_OUT], BF), "rq": ("sbuf", [128, W_OVER], BF),
-    "bp": ("psum", [128, 512], F32), "pn": ("psum", [128, 512], F32), "pf": ("psum", [128, 512], F32),
-    "p2": ("psum", [128, 512], F32), "p3": ("psum", [128, 512], F32),
+    "bp": ("psum", [128, 32, 16], F32), "po": ("psum", [128, 512], F32), "pn": ("psum", [128, 512], F32),
+    "pf": ("psum", [128, 512], F32), "p2": ("psum", [128, 512], F32), "p3": ("psum", [128, 512], F32),
 }
-SEMAPHORES = ["vc", "gi", "ldc", "ldv", "ldi", "ldj", "ms", "msh", "msj", "sb", "sel1", "sel2", "dg", "gd",
-              "rs_o", "rs_n", "rs_f", "lo", "ln", "lfar",
-              "g_e", "g_n", "g_f", "g_f2", "h_n", "h_f", "g_2", "g_j", "g_3a", "g_3b", "t_n", "t_f", "t_2", "t_3",
-              "c_n", "c_f", "c_2", "c_3", "vir0", "vir1", "vir2",
-              "vn", "vf", "gvn", "gvf", "pnr", "pfr", "sent", "sty_a", "sty_b", "rva", "rga", "rpa", "rsent"]
+SEMAPHORES = ["vc", "gi", "ldy", "ldx", "ldi", "ldj", "ms", "msh", "msj", "sb", "sel1", "sel2", "dgr", "dgc", "gd", "lo",
+              "pv", "rs_o", "rs_n", "rs_f", "g_e", "g_n", "g_f", "g_f2", "h_o", "h_n", "h_f", "g_2", "g_j", "g_3a", "g_3b",
+              "t_o", "t_n", "t_f", "t_2", "t_3", "c_o", "c_n", "c_f", "c_2", "c_3", "vir0", "vir1", "vir2",
+              "vn", "vfr", "vfc", "gvn", "gvf", "pnr", "pfr", "sent", "sty_a", "sty_b", "rvra", "rvca", "rga", "rpa",
+              "rsent"]
 
 
 def plan(T, topo):
@@ -79,6 +77,10 @@ def split(topo, a, near, b):
     return leave, [e for e in topo.engines(a, near) if e not in leave]
 
 
+def list_column(T, s, d):
+    return 128 if T.rank_of(s) > T.rank_of(d) else 0
+
+
 def rank_program(g, core, T, topo):
     near, far, out, over = plan(T, topo)
     sem = T.sem
@@ -113,32 +115,44 @@ def rank_program(g, core, T, topo):
             return V.tensor_scalar(out=out, in0=in0, scalar1=s1, scalar2=None, op0=op0)
         return V.tensor_scalar(out=out, in0=in0, scalar1=s1, scalar2=s2, op0=op0, op1=op1)
 
+    lo_n = (8, 24) if up else (0, 16)
+    nr0 = (15, 22) if up else (2, 9)
+    nr1 = (13, 20) if up else (4, 11)
+    nw1 = (11, 22) if up else (2, 13)
+    if edge:
+        lo_f = (7, 16) if up else (8, 17)
+        fr0, fr0b = ((8, 9) if up else (15, 16)), None
+        fr1 = (8, 13) if up else (11, 16)
+        fw1 = (6, 15) if up else (9, 18)
+    else:
+        lo_f = (0, 16) if up else (8, 24)
+        fr0, fr0b = ((4, 9), (2, 4)) if up else ((15, 20), (20, 22))
+        fr1 = (4, 11) if up else (13, 20)
+        fw1 = (2, 16) if up else (9, 22)
+
     cut = 2 * W_OVER
-    SY.dma_start(out=T.v2i[0:64, :], in_=T.vy[:]).then_inc(sem.ldc, 16)
-    S.dma_start(out=T.v2i[64:128, :], in_=T.vx[:]).then_inc(sem.ldc, 16)
-    SY.dma_start(out=T.vyi[:], in_=T.vy[:]).then_inc(sem.ldv, 16)
-    S.dma_start(out=T.vxi[:], in_=T.vx[:]).then_inc(sem.ldv, 16)
+    SY.dma_start(out=T.vyi[:], in_=T.vy[:]).then_inc(sem.ldy, 16)
+    S.dma_start(out=T.vxi[:], in_=T.vx[:]).then_inc(sem.ldx, 16)
     SY.dma_start(out=T.pic[:, 1024:1024 + cut], in_=T.img[:, 0:cut]).then_inc(sem.ldi, 16)
     S.dma_start(out=T.pic[:, 1024 + cut:2048], in_=T.img[:, cut:1024]).then_inc(sem.ldj, 16)
 
     g.iota(out=T.pidx[:], pattern=[[1, 1]], base=0, channel_multiplier=1).then_inc(sem.gi, 1)
-    g.iota(out=T.miota[:], pattern=[[1, 128]], base=0, channel_multiplier=0).then_inc(sem.gi, 1)
     g.iota(out=T.xiota[:], pattern=[[16, 4], [1, 16]], base=0, channel_multiplier=64).then_inc(sem.gi, 1)
-    v(V.memset(T.sel[:], 128.0), "sb")
     v(V.memset(T.jb[:, 0:512], 0.0), "msj")
+    v(V.memset(T.sel[:], 128.0), "sb")
     v(V.memset(T.w0[:, 1024:2048], 0.0), "ms")
     S.wait_ge(sem.msj, 1)
-    for c in (0, 512, 2048, 2560):
+    for c in (2048, 2560, 0, 512) if up else (0, 512, 2048, 2560):
         S.activation(out=T.w0[:, c:c + 512], in_=T.jb[:, 0:512], func=F.Copy).then_inc(sem.msh, 1)
-    V.wait_ge(sem.gi, 3)
-    v(ts(T.pi[:], T.pidx[:], 7, A.bitwise_and))
+    V.wait_ge(sem.gi, 2)
     v(ts(T.hi[:], T.pidx[:], 1, A.arith_shift_right, 7, A.bitwise_and))
     v(ts(T.oi[:], T.pidx[:], 4, A.arith_shift_right, 1, A.bitwise_and))
     if edge:
         v(ts(T.mi[:], T.pidx[:], 15, A.bitwise_and))
-    v(V.tensor_copy(out=T.bp[64:128, 0:128], in_=T.miota[64:128, :]))
+    xi, t1 = T.bp[:, 0:4, :], T.bp[:, 4:8, :]
+    v(V.tensor_copy(out=xi, in_=T.xiota[:]))
     vs()
-    v(ts(T.hrow[:], T.pi[:], float(8 * r + 8), A.add))
+    v(ts(T.hrow[:], T.hi[:], float(8 * r + 8), A.add))
     v(ts(T.h128[:], T.hi[:], 128.0, A.mult, float(128 * (8 * r + 8)), A.add))
     v(ts(T.odd[:], T.oi[:], 1.0, A.mult))
     v(ts(T.even[:], T.oi[:], -1.0, A.mult, 1.0, A.add))
@@ -149,23 +163,36 @@ def rank_program(g, core, T, topo):
     g.wait_ge(sem.sel1, 1)
     g.affine_select(T.sel[:], T.sel[:], pat, A.not_equal, 1.0, -15001, 1).then_inc(sem.sel2, 1)
 
-    V.wait_ge(sem.ldc, 32)
-    v(V.tensor_tensor(out=T.v2i[64:128, :], in0=T.v2i[64:128, :], in1=T.bp[64:128, 0:128], op=A.add))
-    v(ts(T.dig[0:64, :], T.v2i[0:64, :], T.hrow[0:64, 0:1], A.add), "dg")
-    vs()
-    v(ts(T.v2i[64:128, :], T.v2i[64:128, :], 127, A.bitwise_and))
-    vs()
-    v(V.tensor_copy(out=T.dig[64:128, :], in_=T.v2i[64:128, :]), "dg")
-    V.wait_ge(sem.ldv, 32)
-    v(V.tensor_tensor(out=T.ci[:], in0=T.vxi[:], in1=T.xiota[:], op=A.add))
-    v(ts(T.t1[:], T.vyi[:], 128.0, A.mult, T.h128[:, 0:1], A.add))
+    V.wait_ge(sem.ldy, 16)
+    v(ts(T.dig[:, 0:4, :], T.vyi[:], T.hrow[:, 0:1], A.add), "dgr")
+    V.wait_ge(sem.ldx, 16)
+    v(V.tensor_tensor(out=T.ci[:], in0=T.vxi[:], in1=xi, op=A.add))
     vs()
     v(ts(T.ci[:], T.ci[:], 127, A.bitwise_and))
+    v(ts(t1, T.vyi[:], 128.0, A.mult, T.h128[:, 0:1], A.add))
     vs()
-    v(V.tensor_tensor(out=T.gg[:], in0=T.t1[:], in1=T.ci[:], op=A.add), "gd")
+    v(V.tensor_copy(out=T.dig[:, 4:8, :], in_=T.ci[:]), "dgc")
+    v(V.tensor_tensor(out=T.gg[:], in0=t1, in1=T.ci[:], op=A.add))
+    vs()
+    v(ts(T.blk[:, :, 0:16], T.gg[:], T.even[:, 0:1], A.mult))
+    v(ts(T.blk[:, :, 16:32], T.gg[:], T.odd[:, 0:1], A.mult))
+    vs()
+    for b in range(4):
+        v(V.transpose(out=T.tb[:, b:128:4], in_=T.blk[:, b, :]))
+    vs()
+    v(V.tensor_tensor(out=T.lf[:], in0=T.tb[:, 0:64], in1=T.tb[:, 64:128], op=A.add))
+    vs()
+    for lst, d in ((T.lsf, fb), (T.lsn, nb)):
+        if d is not None:
+            first = 8 * T.rank_of(d) + (8 if r > T.rank_of(d) else 0)
+            v(ts(lst[:], T.lf[:], -128.0 * first, A.add), "gd")
+    low = (lo_f if up else lo_n)[0]
+    v(ts(T.l0[:, 72:128], T.lf[:, 8:64], -128.0 * (top + 8), A.add), "lo")
+    v(ts(T.l0[:, 64:72], T.lf[:, 0:8], -128.0 * (top + low), A.add), "lo")
     if edge:
         for k in range(1, 5):
             v(ts(T.kcol[:, k:k + 1], T.mi[:], 0.0, A.is_equal, float(-k if r == 0 else k), A.mult))
+        vs()
 
     es = topo.engines(core, nb)
     ref = core if not edge else nb
@@ -179,60 +206,54 @@ def rank_program(g, core, T, topo):
 
     def image(dst, to, a, b, engines, s):
         send(dst, to, T.pic[:, 1024 + a:1024 + b], engines, s)
-    g.wait_ge(sem.dg, 2)
+    g.wait_ge(sem.dgr, 1)
     if not edge:
-        send(out[(core, fb)][0], T.rv[:], T.dig[:], leave, sem.rva)
+        send(out[(core, fb)][0], T.rvr[:], T.dig[:, 0:4, :], leave, sem.rvra)
+    g.wait_ge(sem.dgc, 1)
+    if not edge:
+        send(out[(core, fb)][0], T.rvc[:], T.dig[:, 4:8, :], leave, sem.rvca)
     send(nb, T.dnear[:], T.dig[:], stay, sem.vn)
-    g.wait_ge(sem.gd, 1)
-    tr = [transfer(topo, core, nb, T.gnear[:], T.gg[:], stay, sem.gvn)]
+    g.wait_ge(sem.gd, 1 if edge else 2)
+    lc = list_column(T, core, nb)
+    tr = [transfer(topo, core, nb, T.l0[:, lc:lc + 64], T.lsn[:], stay, sem.gvn)]
     if not edge:
-        tr.insert(0, transfer(topo, core, out[(core, fb)][0], T.rg[:], T.gg[:], leave, sem.rga))
+        tr.insert(0, transfer(topo, core, out[(core, fb)][0], T.rg[:], T.lsf[:], leave, sem.rga))
     g.remote_dma_fused(tr, local_sem=sem.sent)
     sent[0] += len(tr) * len(stay)
     to = 0 if up else 2048
     g.wait_ge(sem.ldi, 16)
     if edge:
         g.wait_ge(sem.ldj, 16)
+        g.wait_ge(sem.vn, len(stay))
         image(nb, T.pic[:, to:to + 1024], 0, 1024, es, sem.pnr)
     else:
         ro, rw = out[(core, fb)], over[(core, fb)]
         image(rw[0], T.rq[:], *columns("over", 0), leave, sem.rpa)
         g.wait_ge(sem.ldj, 16)
         image(ro[0], T.rp[:], *columns("out", 0), stay, sem.rpa)
+        g.wait_ge(sem.vn, len(stay))
         image(rw[1], T.rq[:], *columns("over", 1), leave, sem.rpa)
         image(ro[1], T.rp[:], *columns("out", 1), stay, sem.rpa)
-        g.wait_ge(sem.rs_n, 32)
+        g.wait_ge(sem.vfc, DIG_ENGINES)
         image(nb, T.pic[:, to:to + cut], 0, cut, stay, sem.pnr)
     pn_inc = len(es) if far.get(nb) is None else (1 + len(out[(nb, far[nb])])) * len(stay)
 
-    def spread(q1, q2, src, col, name):
-        q1.dma_start(out=T.w0[0:128:16, col:col + 1024], in_=src[0:64, :]).then_inc(sem[name], 16)
-        q2.dma_start(out=T.w0[1:128:16, col:col + 1024], in_=src[64:128, :]).then_inc(sem[name], 16)
-    for q in (SY, S):
-        q.wait_ge(sem.ms, 1)
-        q.wait_ge(sem.dg, 2)
-    spread(SY, S, T.dig, 1024, "rs_o")
+    def spread(q, h, src, col, name):
+        q.dma_start(out=T.w0[h:128:16, col:col + 1024], in_=src).then_inc(sem[name], 16)
     ncol, fcol = (2048, 0) if up else (0, 2048)
+    for h, q in enumerate((SY, S)):
+        q.wait_ge(sem.ms, 1)
+        q.wait_ge(sem.dgc if h else sem.dgr, 1)
+        spread(q, h, T.dig[:, 4 * h:4 * h + 4, :], 1024, "rs_o")
     SY.wait_ge(sem.msh, 4)
     SY.wait_ge(sem.vn, len(stay))
-    spread(SY, SY, T.dnear, ncol, "rs_n")
+    for h in range(2):
+        spread(SY, h, T.dnear[:, 4 * h:4 * h + 4, :], ncol, "rs_n")
     if not edge:
-        SY.wait_ge(sem.vf, DIG_ENGINES)
-        spread(SY, SY, T.dfar, fcol, "rs_f")
-
-    def first_list(src, base, outs, name):
-        v(ts(T.blk[:, :, 0:16], src[:], T.even[:, 0:1], A.mult))
-        v(ts(T.blk[:, :, 16:32], src[:], T.odd[:, 0:1], A.mult))
-        vs()
-        for b in range(4):
-            v(V.transpose(out=T.tb[:, b, :], in_=T.blk[:, b, :]))
-        vs()
-        for b in range(4):
-            v(V.tensor_tensor(out=T.lf[:, b:64:4], in0=T.tb[:, b, 0:16], in1=T.tb[:, b, 16:32], op=A.add))
-        vs()
-        for c, m0, m1, add in outs:
-            v(ts(T.l0[:, c:c + m1 - m0], T.lf[:, m0:m1], float(add - 128 * (top + base)), A.add), name)
-        V.wait_ge(sem[name], len(outs))
+        SY.wait_ge(sem.vfr, DIG_ENGINES)
+        spread(SY, 0, T.dfr[:], fcol, "rs_f")
+        SY.wait_ge(sem.vfc, DIG_ENGINES)
+        spread(SY, 1, T.dfc[:], fcol, "rs_f")
 
     def part(eng, out, W, lst, a, b, d, f, name):
         o, i = out[:, 16 * (a - d):16 * (b - d)], W.indirect(lst[:, a - f:b - f])
@@ -254,125 +275,105 @@ def rank_program(g, core, T, topo):
         for q in range(16):
             ins = TE.matmul(ps[:, 0:k], T.sel[:, 15 - q:143 - q], win[:, a + q:b:16], q == 0, q == 15)
         ins.then_inc(sem[name], 1)
-        return k
 
     def both(name, k):
         V.wait_ge(sem[name], k)
         S.wait_ge(sem[name], k)
 
-    if edge:
-        lo_n, lo_f = ((8, 24), (7, 16)) if up else ((0, 16), (8, 17))
-        fr0, fr0b = ((8, 9) if up else (15, 16)), None
-        fr1 = (8, 11) if up else (13, 16)
-        fw1 = (6, 16) if up else (9, 18)
-    else:
-        lo_n, lo_f = ((8, 24), (0, 16)) if up else ((0, 16), (8, 24))
-        fr0, fr0b = ((4, 9), (2, 4)) if up else ((15, 20), (20, 22))
-        fr1 = (4, 11) if up else (13, 20)
-        fw1 = (2, 16) if up else (9, 22)
-    nr0 = (15, 22) if up else (2, 9)
-    nr1 = (11, 20) if up else (4, 13)
-    nw1 = (9, 22) if up else (2, 15)
-    halo = {True: (8, [(128, 0, 48, 0)]), False: (0, [(16, 16, 64, 0)])}
-    low_base = (lo_f if up else lo_n)[0]
+    def listed(lst, rows, ps, base, waits, name):
+        V.wait_ge(sem[waits], 1)
+        v(ts(lst[:, 8 * rows[0]:8 * rows[1]], ps[:, 0:8 * (rows[1] - rows[0])], -128.0 * (top + base), A.add), name)
 
-    V.wait_ge(sem.gd, 1)
-    first_list(T.gg, 8, [(72, 8, 64, 0), (64, 0, 8, 128 * (8 - low_base))], "lo")
-    V.wait_ge(sem.ms, 1)
-    both("msh", 4)
-    S.wait_ge(sem.lo, 2)
-    both("rs_o", 32)
-    gather(T.w1, T.w0, 8, 16, T.l0, (9, 15), 0, "g_e")
-    if edge:
-        a, b = (8, 7) if up else (15, 16)
-        v(ts(T.w0[:, 128 * b:128 * b + 128], T.w0[:, 128 * a:128 * a + 128], T.kcol[:, 1:2], A.add), "vir0")
-
-    V.wait_ge(sem.gvn, len(stay))
-    first_list(T.gnear, halo[up][0], halo[up][1], "ln")
-    S.wait_ge(sem.ln, 1)
-    both("rs_n", 32)
-    gather(T.w1, T.w0, lo_n[0], lo_n[1], T.l0, nr0, 0, "g_n")
-    TE.wait_ge(sem.sel2, 1)
-    TE.wait_ge(sem.g_e, 2)
-    TE.wait_ge(sem.g_n, 2)
-    kn = pick(T.pn, T.w1, nr1, "t_n")
-    V.wait_ge(sem.t_n, 1)
-    v(ts(T.l1[:, 8 * nr1[0]:8 * nr1[1]], T.pn[:, 0:kn], float(-128 * (top + nw1[0])), A.add), "c_n")
-    S.wait_ge(sem.c_n, 1)
-    n0, wn = 8 * nr1[0], T.w1[:, 128 * nw1[0]:128 * nw1[1]]
-    part(S, T.w2, wn, T.l1, n0, n0 + 24, 0, 0, "h_n")
-
-    if not edge:
-        V.wait_ge(sem.gvf, len(topo.engines(out[(fb, core)][0], core)))
-        first_list(T.gfar, halo[not up][0], halo[not up][1], "lfar")
-        S.wait_ge(sem.lfar, 1)
-        both("rs_f", 32)
-    else:
-        both("vir0", 1)
-    gather(T.w1, T.w0, lo_f[0], lo_f[1], T.l0, fr0, 0, "g_f")
-    TE.wait_ge(sem.g_f, 2)
-    kf = pick(T.pf, T.w1, fr1, "t_f")
-    if not edge:
-        gather(T.w1, T.w0, lo_f[0], lo_f[1], T.l0, fr0b, 0, "g_f2")
-    V.wait_ge(sem.c_n, 1)
-    part(V, T.w2, wn, T.l1, n0 + 24, n0 + 48, 0, 0, "h_n")
-    part(S, T.w2, wn, T.l1, n0 + 48, n0 + 72, 0, 0, "h_n")
-
-    def beyond(win, ks, name, wait):
-        V.wait_ge(sem[wait], 2)
+    def beyond(win, ks, name):
         for k in ks:
             a, b = (8, 8 - k) if up else (15, 15 + k)
             v(ts(win[:, 128 * b:128 * b + 128], win[:, 128 * a:128 * a + 128], T.kcol[:, k:k + 1], A.add), name)
-        both(name, len(ks))
 
+    V.wait_ge(sem.ms, 1)
+    both("msh", 4)
+    both("lo", 2)
+    both("rs_o", 32)
+    gather(T.w1, T.w0, 8, 16, T.l0, (9, 15), 0, "g_e")
+    TE.wait_ge(sem.sel2, 1)
+    TE.wait_ge(sem.g_e, 2)
     if edge:
-        beyond(T.w1, (1, 2), "vir1", "g_f")
-    V.wait_ge(sem.t_f, 1)
-    v(ts(T.l1[:, 8 * fr1[0]:8 * fr1[1]], T.pf[:, 0:kf], float(-128 * (top + fw1[0])), A.add), "c_f")
-    both("c_f", 1)
+        beyond(T.w0, (1,), "vir0")
+        both("vir0", 1)
+        gather(T.w1, T.w0, lo_f[0], lo_f[1], T.l0, fr0, 0, "g_f")
+        TE.wait_ge(sem.g_f, 2)
+        pick(T.pf, T.w1, fr1, "t_f")
+        V.wait_ge(sem.g_f, 2)
+        beyond(T.w1, (1, 2), "vir1")
+        both("vir1", 2)
+        both("g_e", 2)
+        both("g_f", 2)
+        listed(T.l1, fr1, T.pf, fw1[0], "t_f", "c_f")
+        S.wait_ge(sem.ldi, 16)
+        S.wait_ge(sem.ldj, 16)
+        a, b = (8, 0) if up else (15, 16)
+        for k in range(8):
+            S.activation(out=T.pic[:, 128 * (b + k):128 * (b + k) + 128], in_=T.pic[:, 128 * a:128 * a + 128],
+                         func=F.Copy).then_inc(sem.pv, 1)
+        both("c_f", 1)
+        gather(T.w2, T.w1, fw1[0], fw1[1], T.l1, fr1, 0, "h_f")
+        V.wait_ge(sem.h_f, 2)
+        beyond(T.w2, (1, 2, 3, 4), "vir2")
+    else:
+        pick(T.po, T.w1, (11, 13), "t_o")
+        listed(T.l1, (11, 13), T.po, 9, "t_o", "c_o")
+        both("c_o", 1)
+        both("g_e", 2)
+        gather(T.w2, T.w1, 9, 15, T.l1, (11, 13), 0, "h_o")
+
+    both("gvn", len(stay))
+    both("rs_n", 32)
+    gather(T.w1, T.w0, lo_n[0], lo_n[1], T.l0, nr0, 0, "g_n")
+    TE.wait_ge(sem.g_n, 2)
+    pick(T.pn, T.w1, nr1, "t_n")
+
     if not edge:
+        both("gvf", len(topo.engines(out[(fb, core)][0], core)))
+        both("rs_f", 32)
+        gather(T.w1, T.w0, lo_f[0], lo_f[1], T.l0, fr0, 0, "g_f")
+        TE.wait_ge(sem.g_f, 2)
+        pick(T.pf, T.w1, fr1, "t_f")
+        gather(T.w1, T.w0, lo_f[0], lo_f[1], T.l0, fr0b, 0, "g_f2")
+    listed(T.l1, nr1, T.pn, nw1[0], "t_n", "c_n")
+    both("c_n", 1)
+    both("g_n", 2)
+    gather(T.w2, T.w1, nw1[0], nw1[1], T.l1, nr1, 0, "h_n")
+    if not edge:
+        listed(T.l1, fr1, T.pf, fw1[0], "t_f", "c_f")
+        both("c_f", 1)
+        both("g_f", 2)
         both("g_f2", 2)
-    gather(T.w2, T.w1, fw1[0], fw1[1], T.l1, fr1, 0, "h_f")
+        gather(T.w2, T.w1, fw1[0], fw1[1], T.l1, fr1, 0, "h_f")
 
     er, fr = ((12, 20), (4, 12)) if up else ((4, 12), (12, 20))
     ew = (8, 24) if up else (0, 16)
-    TE.wait_ge(sem.h_n, 3)
+    TE.wait_ge(sem.h_f if edge else sem.h_o, 2)
+    TE.wait_ge(sem.h_n, 2)
     pick(T.p2, T.w2, er, "t_2")
-    TE.wait_ge(sem.h_f, 2)
     if edge:
-        V.wait_ge(sem.h_n, 3)
-        beyond(T.w2, (1, 2, 3, 4), "vir2", "h_f")
         TE.wait_ge(sem.vir2, 4)
+    else:
+        TE.wait_ge(sem.h_f, 2)
     pick(T.p3, T.w2, fr, "t_3")
     V.wait_ge(sem.t_2, 1)
-    v(ts(T.l2e[:], T.p2[:, 0:64], float(-128 * (top + ew[0])), A.add), "c_2")
-    v(ts(T.l2[:, 8 * er[0]:8 * er[1]], T.p2[:, 0:64], float(-128 * top), A.add), "c_2")
+    v(ts(T.l2e[:], T.p2[:, 0:64], -128.0 * (top + ew[0]), A.add), "c_2")
+    v(ts(T.l2[:, 8 * er[0]:8 * er[1]], T.p2[:, 0:64], -128.0 * top, A.add), "c_2")
     both("c_2", 2)
     both("ldi", 16)
     both("ldj", 16)
     both("pnr", pn_inc)
     gather(T.jb, T.pic, ew[0], ew[1], T.l2e, er, 0, "g_2", er[0])
-    V.wait_ge(sem.t_3, 1)
-    v(ts(T.l2[:, 8 * fr[0]:8 * fr[1]], T.p3[:, 0:64], float(-128 * top), A.add), "c_3")
+    listed(T.l2, fr, T.p3, 0, "t_3", "c_3")
+    both("c_3", 1)
     if edge:
-        v(ts(T.li[:], T.p3[:, 0:64], float(-128 * top), A.add))
-        vs()
-        v(ts(T.la[:], T.li[:], 127, A.bitwise_and))
-        v(ts(T.lb[:], T.li[:], 7, A.arith_shift_right))
-        vs()
-        v(ts(T.lb[:], T.lb[:], 8.0 if up else 15.0, A.max if up else A.min, -float(ew[0]), A.add))
-        vs()
-        v(ts(T.li[:], T.lb[:], 128.0, A.mult))
-        vs()
-        v(V.tensor_tensor(out=T.li[:], in0=T.li[:], in1=T.la[:], op=A.add))
-        vs()
-        v(V.tensor_copy(out=T.l3[:], in_=T.li[:]), "c_3")
-    both("c_3", 2 if edge else 1)
-    if edge:
-        gather(T.jb, T.pic, ew[0], ew[1], T.l3, fr, 0, "g_j", fr[0])
+        both("pv", 8)
     else:
         both("pfr", sum(len(topo.engines(x, core)) for x in out[(fb, core)] + over[(fb, core)]))
-        gather(T.jb, T.pic, 0, 24, T.l2, fr, 0, "g_j")
+    gather(T.jb, T.pic, 0, 24, T.l2, fr, 0, "g_j")
     both("g_2", 2)
     both("g_j", 2)
     both("msj", 1)
@@ -382,7 +383,6 @@ def rank_program(g, core, T, topo):
     SY.dma_start(out=T.y[:, 0:512], in_=T.yo[:, 0:512]).then_inc(sem.sty_a, 16)
     S.wait_ge(sem.g_3b, 2)
     S.dma_start(out=T.y[:, 512:1024], in_=T.yo[:, 512:1024]).then_inc(sem.sty_b, 16)
-    vs()
     g.wait_ge(sem.sent, sent[0])
     g.wait_ge(sem.sty_a, 16)
     g.wait_ge(sem.sty_b, 16)
@@ -390,28 +390,38 @@ def rank_program(g, core, T, topo):
 
 def hand_on(g, core, T, topo, s, d, way, i, nb):
     sem = T.sem
-    rid, pid = topo.addr(d, core)
     m, ne = topo.mask(core, d), len(topo.engines(core, d))
     es = topo.engines(s, core)
     a, b = columns(way, i)
-    o = 0 if T.rank_of(d) > T.rank_of(s) else 2048
+
+    def pass_on(dst, to, held, arrived, mask):
+        rid, pid = topo.addr(dst, core)
+        g.remote_dma(to, held, arrived, sem.rsent, pid, rid, mask)
+
+    def image(dst, held, arrived, mask):
+        o = 0 if T.rank_of(dst) > T.rank_of(s) else 2048
+        pass_on(dst, T.pic[:, o + a:o + b], held, arrived, mask)
     if way == "over":
         g.wait_ge(sem.rpa, len(es))
-        g.remote_dma(T.pic[:, o + a:o + b], T.rq[:], sem.pfr, sem.rsent, pid, rid, m)
+        image(d, T.rq[:], sem.pfr, m)
         g.wait_ge(sem.rsent, ne)
         return
     leave, stay = split(topo, core, nb, d)
     n = ne + len(stay)
     half = len(es) // 2
     if i == 0:
-        g.wait_ge(sem.rva, half)
-        g.remote_dma(T.dfar[:], T.rv[:], sem.vf, sem.rsent, pid, rid, bits(leave[:DIG_ENGINES]))
+        g.wait_ge(sem.rvra, half)
+        pass_on(d, T.dfr[:], T.rvr[:], sem.vfr, bits(leave[:DIG_ENGINES]))
+        g.wait_ge(sem.rvca, half)
+        pass_on(d, T.dfc[:], T.rvc[:], sem.vfc, bits(leave[:DIG_ENGINES]))
         g.wait_ge(sem.rga, half)
-        g.remote_dma(T.gfar[:], T.rg[:], sem.gvf, sem.rsent, pid, rid, m)
-        n += DIG_ENGINES + ne
+        lc = list_column(T, s, d)
+        pass_on(d, T.l0[:, lc:lc + 64], T.rg[:], sem.gvf, m)
+        n += 2 * DIG_ENGINES + ne
     g.wait_ge(sem.rpa, half)
-    g.remote_dma(T.pic[:, o + a:o + b], T.rp[:], sem.pfr, sem.rsent, pid, rid, m)
-    o = 0 if T.rank_of(nb) > T.rank_of(s) else 2048
-    rid, pid = topo.addr(nb, core)
-    g.remote_dma(T.pic[:, o + a:o + b], T.rp[:], sem.pnr, sem.rsent, pid, rid, bits(stay))
+    if i == 0:
+        image(d, T.rp[:], sem.pfr, m)
+    image(nb, T.rp[:], sem.pnr, bits(stay))
+    if i == 1:
+        image(d, T.rp[:], sem.pfr, m)
     g.wait_ge(sem.rsent, n)

@@ -11,12 +11,14 @@ SCRATCH = {
     "oi": ("sbuf", [128, 1], I32), "mi": ("sbuf", [128, 1], I32),
     "hrow": ("sbuf", [128, 1], F32), "h128": ("sbuf", [128, 1], F32),
     "odd": ("sbuf", [128, 1], F32), "even": ("sbuf", [128, 1], F32), "kcol": ("sbuf", [128, 8], F32),
-    "dig": ("sbuf", [128, 8, 16], BF), "dnear": ("sbuf", [128, 8, 16], BF),
+    "dig": ("sbuf", [128, 8, 16], BF),
+    "dnr": ("dram", [128, 4, 16], BF), "dnc": ("dram", [128, 4, 16], BF),
     "dfr": ("dram", [128, 4, 16], BF), "dfc": ("dram", [128, 4, 16], BF),
     "gg": ("sbuf", [128, 4, 16], F32), "blk": ("sbuf", [128, 4, 32], F32), "tb": ("sbuf", [128, 128], F32),
     "lf": ("sbuf", [128, 64], F32), "lsn": ("sbuf", [128, 64], U16), "lsf": ("sbuf", [128, 64], U16),
+    "ln1": ("sbuf", [128, 48], U16), "lf1": ("sbuf", [128, 48], U16), "rh": ("sbuf", [128, 48], U16),
     "l0": ("sbuf", [128, 192], U16), "l1": ("sbuf", [128, 192], U16), "l2": ("sbuf", [128, 192], U16),
-    "l2e": ("sbuf", [128, 64], U16),
+    "l2e": ("sbuf", [128, 192], U16), "l3": ("sbuf", [128, 192], U16),
     "w0": ("sbuf", [128, 3072], BF), "w1": ("sbuf", [128, 3072], BF), "w2": ("sbuf", [128, 3072], BF),
     "jb": ("sbuf", [128, 3072], BF), "pic": ("sbuf", [128, 3072], BF), "yo": ("sbuf", [128, 1024], BF),
     "sel": ("sbuf", [128, 144], BF),
@@ -26,10 +28,10 @@ SCRATCH = {
     "pf": ("psum", [128, 512], F32), "p2": ("psum", [128, 512], F32), "p3": ("psum", [128, 512], F32),
 }
 SEMAPHORES = ["vc", "gi", "ldy", "ldx", "ldi", "ldj", "ms", "msh", "msj", "sb", "sel1", "sel2", "dgr", "dgc", "gd", "lo",
-              "pv", "rs_o", "rs_n", "rs_f", "g_e", "g_n", "g_f", "g_f2", "h_o", "h_n", "h_f", "g_2", "g_j", "g_3a", "g_3b",
-              "t_o", "t_n", "t_f", "t_2", "t_3", "c_o", "c_n", "c_f", "c_2", "c_3", "vir0", "vir1", "vir2",
+              "pv", "rs_o", "rs_n", "rs_f", "g_e", "g_n", "g_f", "g_f2", "h_o", "h_m", "h_n", "h_f", "g_2", "g_j", "g_3a",
+              "g_3b", "t_o", "t_n", "t_f", "t_2", "t_3", "c_o", "c_n", "c_f", "c_2", "c_2b", "c_3", "vir0", "vir1", "vir2",
               "vn", "vfr", "vfc", "gvn", "gvf", "pnr", "pfr", "sent", "sty_a", "sty_b", "rvra", "rvca", "rga", "rpa",
-              "rsent"]
+              "rsent", "gd1", "l1n", "l1f", "rha"]
 
 
 def plan(T, topo):
@@ -115,26 +117,35 @@ def rank_program(g, core, T, topo):
             return V.tensor_scalar(out=out, in0=in0, scalar1=s1, scalar2=None, op0=op0)
         return V.tensor_scalar(out=out, in0=in0, scalar1=s1, scalar2=s2, op0=op0, op1=op1)
 
+    def near_window(u):
+        return (11, 22) if u else (2, 13)
+
+    def far_window(u):
+        return (2, 16) if u else (9, 22)
     lo_n = (8, 24) if up else (0, 16)
     nr0 = (15, 22) if up else (2, 9)
-    nr1 = (13, 20) if up else (4, 11)
-    nw1 = (11, 22) if up else (2, 13)
+    nr1 = (15, 17) if up else (7, 9)
+    nra = (13, 15) if up else (9, 11)
+    nrb = (17, 20) if up else (4, 7)
+    nw1 = near_window(up)
     if edge:
         lo_f = (7, 16) if up else (8, 17)
-        fr0, fr0b = ((8, 9) if up else (15, 16)), None
+        fr0 = (8, 9) if up else (15, 16)
         fr1 = (8, 13) if up else (11, 16)
+        hf = fr1
         fw1 = (6, 15) if up else (9, 18)
     else:
         lo_f = (0, 16) if up else (8, 24)
-        fr0, fr0b = ((4, 9), (2, 4)) if up else ((15, 20), (20, 22))
-        fr1 = (4, 11) if up else (13, 20)
-        fw1 = (2, 16) if up else (9, 22)
+        fr0, fr0b = ((7, 9), (2, 7)) if up else ((15, 17), (17, 22))
+        fr1 = fr0
+        fra = (9, 11) if up else (13, 15)
+        hf = (4, 11) if up else (13, 20)
+        fw1 = far_window(up)
 
     cut = 2 * W_OVER
     SY.dma_start(out=T.vyi[:], in_=T.vy[:]).then_inc(sem.ldy, 16)
-    S.dma_start(out=T.vxi[:], in_=T.vx[:]).then_inc(sem.ldx, 16)
+    SY.dma_start(out=T.vxi[:], in_=T.vx[:]).then_inc(sem.ldx, 16)
     SY.dma_start(out=T.pic[:, 1024:1024 + cut], in_=T.img[:, 0:cut]).then_inc(sem.ldi, 16)
-    S.dma_start(out=T.pic[:, 1024 + cut:2048], in_=T.img[:, cut:1024]).then_inc(sem.ldj, 16)
 
     g.iota(out=T.pidx[:], pattern=[[1, 1]], base=0, channel_multiplier=1).then_inc(sem.gi, 1)
     g.iota(out=T.xiota[:], pattern=[[16, 4], [1, 16]], base=0, channel_multiplier=64).then_inc(sem.gi, 1)
@@ -142,6 +153,7 @@ def rank_program(g, core, T, topo):
     v(V.memset(T.sel[:], 128.0), "sb")
     v(V.memset(T.w0[:, 1024:2048], 0.0), "ms")
     S.wait_ge(sem.msj, 1)
+    S.dma_start(out=T.pic[:, 1024 + cut:2048], in_=T.img[:, cut:1024]).then_inc(sem.ldj, 16)
     for c in (2048, 2560, 0, 512) if up else (0, 512, 2048, 2560):
         S.activation(out=T.w0[:, c:c + 512], in_=T.jb[:, 0:512], func=F.Copy).then_inc(sem.msh, 1)
     V.wait_ge(sem.gi, 2)
@@ -204,6 +216,10 @@ def rank_program(g, core, T, topo):
         g.remote_dma(to, src, s, sem.sent, pid, rid, bits(engines))
         sent[0] += len(engines)
 
+    def fused(tr):
+        g.remote_dma_fused(tr, local_sem=sem.sent)
+        sent[0] += len(tr) * len(stay)
+
     def image(dst, to, a, b, engines, s):
         send(dst, to, T.pic[:, 1024 + a:1024 + b], engines, s)
     g.wait_ge(sem.dgr, 1)
@@ -212,28 +228,34 @@ def rank_program(g, core, T, topo):
     g.wait_ge(sem.dgc, 1)
     if not edge:
         send(out[(core, fb)][0], T.rvc[:], T.dig[:, 4:8, :], leave, sem.rvca)
-    send(nb, T.dnear[:], T.dig[:], stay, sem.vn)
-    g.wait_ge(sem.gd, 1 if edge else 2)
+    fused([transfer(topo, core, nb, T.dnr[:], T.dig[:, 0:4, :], stay, sem.vn),
+           transfer(topo, core, nb, T.dnc[:], T.dig[:, 4:8, :], leave, sem.vn)])
     lc = list_column(T, core, nb)
-    tr = [transfer(topo, core, nb, T.l0[:, lc:lc + 64], T.lsn[:], stay, sem.gvn)]
-    if not edge:
-        tr.insert(0, transfer(topo, core, out[(core, fb)][0], T.rg[:], T.lsf[:], leave, sem.rga))
-    g.remote_dma_fused(tr, local_sem=sem.sent)
-    sent[0] += len(tr) * len(stay)
+
+    def lists(ready, name, here, there, at, a, b, relayed):
+        g.wait_ge(sem[ready], 1 if edge else 2)
+        tr = [transfer(topo, core, nb, at[:, a:b], here, stay, sem[name])]
+        if not edge:
+            tr.insert(0, transfer(topo, core, out[(core, fb)][0], relayed[0], there, leave, relayed[1]))
+        fused(tr)
+    lists("gd", "gvn", T.lsn[:], T.lsf[:], T.l0, lc, lc + 64, (T.rg[:], sem.rga))
     to = 0 if up else 2048
     g.wait_ge(sem.ldi, 16)
+    second = ("gd1", "l1n", T.ln1[:], T.lf1[:], T.l1, lc + 8, lc + 56, (T.rh[:], sem.rha))
     if edge:
         g.wait_ge(sem.ldj, 16)
-        g.wait_ge(sem.vn, len(stay))
+        g.wait_ge(sem.vn, len(es))
         image(nb, T.pic[:, to:to + 1024], 0, 1024, es, sem.pnr)
+        lists(*second)
     else:
         ro, rw = out[(core, fb)], over[(core, fb)]
         image(rw[0], T.rq[:], *columns("over", 0), leave, sem.rpa)
         g.wait_ge(sem.ldj, 16)
         image(ro[0], T.rp[:], *columns("out", 0), stay, sem.rpa)
-        g.wait_ge(sem.vn, len(stay))
+        g.wait_ge(sem.vn, len(es))
         image(rw[1], T.rq[:], *columns("over", 1), leave, sem.rpa)
         image(ro[1], T.rp[:], *columns("out", 1), stay, sem.rpa)
+        lists(*second)
         g.wait_ge(sem.vfc, DIG_ENGINES)
         image(nb, T.pic[:, to:to + cut], 0, cut, stay, sem.pnr)
     pn_inc = len(es) if far.get(nb) is None else (1 + len(out[(nb, far[nb])])) * len(stay)
@@ -246,28 +268,27 @@ def rank_program(g, core, T, topo):
         q.wait_ge(sem.dgc if h else sem.dgr, 1)
         spread(q, h, T.dig[:, 4 * h:4 * h + 4, :], 1024, "rs_o")
     SY.wait_ge(sem.msh, 4)
-    SY.wait_ge(sem.vn, len(stay))
-    for h in range(2):
-        spread(SY, h, T.dnear[:, 4 * h:4 * h + 4, :], ncol, "rs_n")
+    SY.wait_ge(sem.vn, len(es))
+    spread(SY, 0, T.dnr[:], ncol, "rs_n")
+    spread(SY, 1, T.dnc[:], ncol, "rs_n")
     if not edge:
         SY.wait_ge(sem.vfr, DIG_ENGINES)
         spread(SY, 0, T.dfr[:], fcol, "rs_f")
         SY.wait_ge(sem.vfc, DIG_ENGINES)
         spread(SY, 1, T.dfc[:], fcol, "rs_f")
 
-    def part(eng, out, W, lst, a, b, d, f, name):
-        o, i = out[:, 16 * (a - d):16 * (b - d)], W.indirect(lst[:, a - f:b - f])
+    def part(eng, out, W, lst, a, b, d, name):
+        o, i = out[:, 16 * (a - d):16 * (b - d)], W.indirect(lst[:, a:b])
         if eng is V:
             V.tensor_copy(out=o, in_=i).then_inc(sem[name], 1)
         else:
             S.activation(out=o, in_=i, func=F.Copy).then_inc(sem[name], 1)
 
-    def gather(out, win, lo, hi, lst, rows, o0, name, l0=None):
+    def gather(out, win, w, lst, rows, name, o0=0):
         a, b = 8 * rows[0], 8 * rows[1]
         m = a + (b - a) // 4 * 2
-        d, f = 8 * o0, 8 * (o0 if l0 is None else l0)
-        part(V, out, win[:, 128 * lo:128 * hi], lst, a, m, d, f, name)
-        part(S, out, win[:, 128 * lo:128 * hi], lst, m, b, d, f, name)
+        part(V, out, win[:, 128 * w[0]:128 * w[1]], lst, a, m, 8 * o0, name)
+        part(S, out, win[:, 128 * w[0]:128 * w[1]], lst, m, b, 8 * o0, name)
 
     def pick(ps, win, rows, name):
         a, b = 128 * rows[0], 128 * rows[1]
@@ -293,92 +314,114 @@ def rank_program(g, core, T, topo):
     both("msh", 4)
     both("lo", 2)
     both("rs_o", 32)
-    gather(T.w1, T.w0, 8, 16, T.l0, (9, 15), 0, "g_e")
+    gather(T.w1, T.w0, (8, 16), T.l0, (9, 15), "g_e")
     TE.wait_ge(sem.sel2, 1)
     TE.wait_ge(sem.g_e, 2)
+    pick(T.po, T.w1, (9, 15), "t_o")
     if edge:
         beyond(T.w0, (1,), "vir0")
         both("vir0", 1)
-        gather(T.w1, T.w0, lo_f[0], lo_f[1], T.l0, fr0, 0, "g_f")
+        gather(T.w1, T.w0, lo_f, T.l0, fr0, "g_f")
         TE.wait_ge(sem.g_f, 2)
         pick(T.pf, T.w1, fr1, "t_f")
         V.wait_ge(sem.g_f, 2)
         beyond(T.w1, (1, 2), "vir1")
+    V.wait_ge(sem.t_o, 1)
+    for lst, d, window in ((T.lf1, fb, far_window), (T.ln1, nb, near_window)):
+        if d is not None:
+            first = 8 * T.rank_of(d) + window(T.rank_of(near[d]) > T.rank_of(d))[0]
+            v(ts(lst[:], T.po[:, 0:48], -128.0 * first, A.add), "gd1")
+    own = [(nra, nw1[0])] if edge else [((11, 13), 9), (nra, nw1[0]), (fra, fw1[0])]
+    for (a, b), base in own:
+        v(ts(T.l1[:, 8 * a:8 * b], T.po[:, 8 * (a - 9):8 * (b - 9)], -128.0 * (top + base), A.add), "c_o")
+    both("c_o", len(own))
+    both("g_e", 2)
+    if edge:
         both("vir1", 2)
-        both("g_e", 2)
         both("g_f", 2)
-        listed(T.l1, fr1, T.pf, fw1[0], "t_f", "c_f")
-        S.wait_ge(sem.ldi, 16)
-        S.wait_ge(sem.ldj, 16)
-        a, b = (8, 0) if up else (15, 16)
-        for k in range(8):
-            S.activation(out=T.pic[:, 128 * (b + k):128 * (b + k) + 128], in_=T.pic[:, 128 * a:128 * a + 128],
-                         func=F.Copy).then_inc(sem.pv, 1)
+        listed(T.l1, fr1 if up else (11, 13), T.pf, fw1[0], "t_f", "c_f") if False else None
+        V.wait_ge(sem.t_f, 1)
+        v(ts(T.l3[:, 8 * fr1[0]:8 * fr1[1]], T.pf[:, 0:40], -128.0 * (top + fw1[0]), A.add), "c_f")
         both("c_f", 1)
-        gather(T.w2, T.w1, fw1[0], fw1[1], T.l1, fr1, 0, "h_f")
-        V.wait_ge(sem.h_f, 2)
-        beyond(T.w2, (1, 2, 3, 4), "vir2")
+        gather(T.w2, T.w1, fw1, T.l3, fr1, "h_f")
     else:
-        pick(T.po, T.w1, (11, 13), "t_o")
-        listed(T.l1, (11, 13), T.po, 9, "t_o", "c_o")
-        both("c_o", 1)
-        both("g_e", 2)
-        gather(T.w2, T.w1, 9, 15, T.l1, (11, 13), 0, "h_o")
+        gather(T.w2, T.w1, (9, 15), T.l1, (11, 13), "h_o")
 
     both("gvn", len(stay))
     both("rs_n", 32)
-    gather(T.w1, T.w0, lo_n[0], lo_n[1], T.l0, nr0, 0, "g_n")
+    gather(T.w1, T.w0, lo_n, T.l0, nr0, "g_n")
     TE.wait_ge(sem.g_n, 2)
     pick(T.pn, T.w1, nr1, "t_n")
-
-    if not edge:
+    er, fr = ((12, 20), (4, 12)) if up else ((4, 12), (12, 20))
+    ew = (8, 24) if up else (0, 16)
+    if edge:
+        V.wait_ge(sem.h_f, 2)
+        beyond(T.w2, (1, 2, 3, 4), "vir2")
+        TE.wait_ge(sem.h_f, 2)
+        TE.wait_ge(sem.vir2, 4)
+        both("ldi", 16)
+        both("ldj", 16)
+        a, b = (8, 0) if up else (15, 16)
+        for k in range(8):
+            v(V.tensor_copy(out=T.pic[:, 128 * (b + k):128 * (b + k) + 128], in_=T.pic[:, 128 * a:128 * a + 128]), "pv")
+    both("g_n", 2)
+    both("l1n", len(stay))
+    if edge:
+        gather(T.w2, T.w1, nw1, T.l1, nra, "h_m")
+        gather(T.w2, T.w1, nw1, T.l1, nrb, "h_m")
+        pick(T.p3, T.w2, fr, "t_3")
+    else:
+        gather(T.w2, T.w1, nw1, T.l1, nra, "h_m")
+        gather(T.w2, T.w1, nw1, T.l1, nrb, "h_m")
         both("gvf", len(topo.engines(out[(fb, core)][0], core)))
         both("rs_f", 32)
-        gather(T.w1, T.w0, lo_f[0], lo_f[1], T.l0, fr0, 0, "g_f")
+        gather(T.w1, T.w0, lo_f, T.l0, fr0, "g_f")
         TE.wait_ge(sem.g_f, 2)
         pick(T.pf, T.w1, fr1, "t_f")
-        gather(T.w1, T.w0, lo_f[0], lo_f[1], T.l0, fr0b, 0, "g_f2")
     listed(T.l1, nr1, T.pn, nw1[0], "t_n", "c_n")
+    if not edge:
+        gather(T.w1, T.w0, lo_f, T.l0, fr0b, "g_f2")
     both("c_n", 1)
-    both("g_n", 2)
-    gather(T.w2, T.w1, nw1[0], nw1[1], T.l1, nr1, 0, "h_n")
+    gather(T.w2, T.w1, nw1, T.l1, nr1, "h_n")
     if not edge:
         listed(T.l1, fr1, T.pf, fw1[0], "t_f", "c_f")
         both("c_f", 1)
         both("g_f", 2)
         both("g_f2", 2)
-        gather(T.w2, T.w1, fw1[0], fw1[1], T.l1, fr1, 0, "h_f")
+        both("l1f", len(topo.engines(out[(fb, core)][0], core)))
+        gather(T.w2, T.w1, fw1, T.l1, hf, "h_f")
 
-    er, fr = ((12, 20), (4, 12)) if up else ((4, 12), (12, 20))
-    ew = (8, 24) if up else (0, 16)
     TE.wait_ge(sem.h_f if edge else sem.h_o, 2)
+    TE.wait_ge(sem.h_m, 4)
     TE.wait_ge(sem.h_n, 2)
     pick(T.p2, T.w2, er, "t_2")
     if edge:
-        TE.wait_ge(sem.vir2, 4)
-    else:
-        TE.wait_ge(sem.h_f, 2)
-    pick(T.p3, T.w2, fr, "t_3")
-    V.wait_ge(sem.t_2, 1)
-    v(ts(T.l2e[:], T.p2[:, 0:64], -128.0 * (top + ew[0]), A.add), "c_2")
-    v(ts(T.l2[:, 8 * er[0]:8 * er[1]], T.p2[:, 0:64], -128.0 * top, A.add), "c_2")
-    both("c_2", 2)
+        gw = (0, 16) if up else (8, 24)
+        listed(T.l2e, fr, T.p3, gw[0], "t_3", "c_3")
+        both("c_3", 1)
+        both("pv", 8)
+        gather(T.jb, T.pic, gw, T.l2e, fr, "g_j")
+        v(ts(T.l2[:, 8 * fr[0]:8 * fr[1]], T.p3[:, 0:64], -128.0 * top, A.add), "c_2b")
+    listed(T.l2e, er, T.p2, ew[0], "t_2", "c_2")
+    both("c_2", 1)
     both("ldi", 16)
     both("ldj", 16)
     both("pnr", pn_inc)
-    gather(T.jb, T.pic, ew[0], ew[1], T.l2e, er, 0, "g_2", er[0])
-    listed(T.l2, fr, T.p3, 0, "t_3", "c_3")
-    both("c_3", 1)
-    if edge:
-        both("pv", 8)
-    else:
+    gather(T.jb, T.pic, ew, T.l2e, er, "g_2")
+    if not edge:
+        TE.wait_ge(sem.h_f, 2)
+        pick(T.p3, T.w2, fr, "t_3")
+        listed(T.l2, fr, T.p3, 0, "t_3", "c_3")
+        both("c_3", 1)
         both("pfr", sum(len(topo.engines(x, core)) for x in out[(fb, core)] + over[(fb, core)]))
-    gather(T.jb, T.pic, 0, 24, T.l2, fr, 0, "g_j")
+        gather(T.jb, T.pic, (0, 24), T.l2, fr, "g_j")
+    v(ts(T.l2[:, 8 * er[0]:8 * er[1]], T.p2[:, 0:64], -128.0 * top, A.add), "c_2b")
     both("g_2", 2)
     both("g_j", 2)
+    both("c_2b", 2 if edge else 1)
     both("msj", 1)
-    gather(T.yo, T.jb, 0, 20, T.l2, (8, 12), 8, "g_3a", 0)
-    gather(T.yo, T.jb, 0, 20, T.l2, (12, 16), 8, "g_3b", 0)
+    gather(T.yo, T.jb, (0, 20), T.l2, (8, 12), "g_3a", 8)
+    gather(T.yo, T.jb, (0, 20), T.l2, (12, 16), "g_3b", 8)
     SY.wait_ge(sem.g_3a, 2)
     SY.dma_start(out=T.y[:, 0:512], in_=T.yo[:, 0:512]).then_inc(sem.sty_a, 16)
     S.wait_ge(sem.g_3b, 2)
@@ -409,19 +452,22 @@ def hand_on(g, core, T, topo, s, d, way, i, nb):
     leave, stay = split(topo, core, nb, d)
     n = ne + len(stay)
     half = len(es) // 2
+    lc = list_column(T, s, d)
     if i == 0:
         g.wait_ge(sem.rvra, half)
         pass_on(d, T.dfr[:], T.rvr[:], sem.vfr, bits(leave[:DIG_ENGINES]))
         g.wait_ge(sem.rvca, half)
         pass_on(d, T.dfc[:], T.rvc[:], sem.vfc, bits(leave[:DIG_ENGINES]))
         g.wait_ge(sem.rga, half)
-        lc = list_column(T, s, d)
         pass_on(d, T.l0[:, lc:lc + 64], T.rg[:], sem.gvf, m)
-        n += 2 * DIG_ENGINES + ne
+        n += 2 * DIG_ENGINES + 2 * ne
     g.wait_ge(sem.rpa, half)
     if i == 0:
         image(d, T.rp[:], sem.pfr, m)
     image(nb, T.rp[:], sem.pnr, bits(stay))
-    if i == 1:
+    if i == 0:
+        g.wait_ge(sem.rha, half)
+        pass_on(d, T.l1[:, lc + 8:lc + 56], T.rh[:], sem.l1f, m)
+    else:
         image(d, T.rp[:], sem.pfr, m)
     g.wait_ge(sem.rsent, n)

from concourse.bass import DstId, RemoteDMATransfer
from concourse.mybir import AluOpType as A, ActivationFunctionType as F

BF, F32, I32, U16 = "bfloat16", "float32", "int32", "uint16"
SIM_CORES = 256
W_OUT, W_OVER = 320, 192
DIG_ENGINES = 4
SCRATCH = {
    "vyi": ("sbuf", [128, 4, 16], I32), "vxi": ("sbuf", [128, 4, 16], I32), "ci": ("sbuf", [128, 4, 16], I32),
    "xiota": ("sbuf", [128, 4, 16], I32), "pidx": ("sbuf", [128, 1], I32), "hi": ("sbuf", [128, 1], I32),
    "oi": ("sbuf", [128, 1], I32), "mi": ("sbuf", [128, 1], I32),
    "hrow": ("sbuf", [128, 1], F32), "h128": ("sbuf", [128, 1], F32),
    "odd": ("sbuf", [128, 1], F32), "even": ("sbuf", [128, 1], F32), "kcol": ("sbuf", [128, 8], F32),
    "dig": ("sbuf", [128, 8, 16], BF),
    "dnr": ("dram", [128, 4, 16], BF), "dnc": ("dram", [128, 4, 16], BF),
    "dfr": ("dram", [128, 4, 16], BF), "dfc": ("dram", [128, 4, 16], BF),
    "gg": ("sbuf", [128, 4, 16], F32), "blk": ("sbuf", [128, 4, 32], F32), "tb": ("sbuf", [128, 128], F32),
    "lf": ("sbuf", [128, 64], F32), "lsn": ("sbuf", [128, 64], U16), "lsf": ("sbuf", [128, 64], U16),
    "ln1": ("sbuf", [128, 48], U16), "lf1": ("sbuf", [128, 48], U16), "rh": ("sbuf", [128, 48], U16),
    "l0": ("sbuf", [128, 192], U16), "l1": ("sbuf", [128, 192], U16), "l2": ("sbuf", [128, 192], U16),
    "l2e": ("sbuf", [128, 192], U16), "l3": ("sbuf", [128, 192], U16),
    "w0": ("sbuf", [128, 3072], BF), "w1": ("sbuf", [128, 3072], BF), "w2": ("sbuf", [128, 3072], BF),
    "jb": ("sbuf", [128, 3072], BF), "pic": ("sbuf", [128, 3072], BF), "yo": ("sbuf", [128, 1024], BF),
    "sel": ("sbuf", [128, 144], BF),
    "rvr": ("dram", [128, 4, 16], BF), "rvc": ("dram", [128, 4, 16], BF), "rg": ("sbuf", [128, 64], U16),
    "rp": ("sbuf", [128, W_OUT], BF), "rq": ("sbuf", [128, W_OVER], BF),
    "bp": ("psum", [128, 32, 16], F32), "po": ("psum", [128, 512], F32), "pn": ("psum", [128, 512], F32),
    "pf": ("psum", [128, 512], F32), "p2": ("psum", [128, 512], F32), "p3": ("psum", [128, 512], F32),
}
SEMAPHORES = ["vc", "gi", "ldy", "ldx", "ldi", "ldj", "ms", "msh", "msj", "sb", "sel1", "sel2", "dgr", "dgc", "gd", "lo",
              "pv", "rs_o", "rs_n", "rs_f", "g_e", "g_n", "g_f", "g_f2", "h_o", "h_m", "h_n", "h_f", "g_2", "g_j", "g_3a",
              "g_3b", "t_o", "t_n", "t_f", "t_2", "t_3", "c_o", "c_n", "c_f", "c_2", "c_2b", "c_3", "vir0", "vir1", "vir2",
              "vn", "vfr", "vfc", "gvn", "gvf", "pnr", "pfr", "sent", "sty_a", "sty_b", "rvra", "rvca", "rga", "rpa",
              "rsent", "gd1", "l1n", "l1f", "rha"]


def plan(T, topo):
    cs = list(T.cores)
    near, far, flows = {}, {}, []
    for a, b in zip(cs, cs[1:]):
        if b in topo.cores_of(a):
            near[a], near[b] = b, a
        else:
            far[a], far[b] = b, a
            flows += [(a, b), (b, a)]
    out, over, used = {}, {}, set()
    for s, d in flows:
        for way, c in ((out, topo.cores_of(s)), (over, [x for x in range(SIM_CORES) if topo.mates(x, d)])):
            pair = []
            for e in (topo.die(s), 1 - topo.die(s)):
                x = [x for x in c if T.rank_of(x) is None and x not in used and topo.die(x) == e
                     and topo.may_write(x, d) and topo.may_write(s, x)][0]
                used.add(x)
                pair.append(x)
            way[(s, d)] = pair
    return near, far, out, over


def bits(engines):
    m = 0
    for e in engines:
        m |= 1 << e
    return m


def transfer(topo, src, dst, out, in_, engines, sem):
    rid, pid = topo.addr(dst, src)
    return RemoteDMATransfer(dst_ids=[DstId(rid=rid, pnc=pid)], dma_engine_mask=bits(engines), remote_sem=sem,
                             src=in_, dst=out)


def columns(way, i):
    a = i * W_OVER if way == "over" else 2 * W_OVER + i * W_OUT
    return a, a + (W_OVER if way == "over" else W_OUT)


def split(topo, a, near, b):
    leave = topo.engines(a, b)
    return leave, [e for e in topo.engines(a, near) if e not in leave]


def list_column(T, s, d):
    return 128 if T.rank_of(s) > T.rank_of(d) else 0


def rank_program(g, core, T, topo):
    near, far, out, over = plan(T, topo)
    sem = T.sem
    if T.rank_of(core) is None:
        for name, way in (("out", out), ("over", over)):
            for (s, d), rel in way.items():
                if core in rel:
                    hand_on(g, core, T, topo, s, d, name, rel.index(core), near[s])
        return
    r = T.rank_of(core)
    nb, fb = near[core], far.get(core)
    up = T.rank_of(nb) > r
    edge = fb is None
    V, S, TE, SY = g.vector, g.scalar, g.tensor, g.sync
    top = 8 * r
    cnt = [0, 0]

    def v(ins, name=None):
        if name:
            ins.then_inc(sem[name], 1)
        else:
            ins.then_inc(sem.vc, 1)
            cnt[0] += 1

    def vs():
        if cnt[0] > cnt[1]:
            V.wait_ge(sem.vc, cnt[0])
            cnt[1] = cnt[0]

    def ts(out, in0, s1, op0, s2=None, op1=None):
        if op1 is None:
            return V.tensor_scalar(out=out, in0=in0, scalar1=s1, scalar2=None, op0=op0)
        return V.tensor_scalar(out=out, in0=in0, scalar1=s1, scalar2=s2, op0=op0, op1=op1)

    def near_window(u):
        return (11, 22) if u else (2, 13)

    def far_window(u):
        return (2, 16) if u else (9, 22)
    lo_n = (8, 24) if up else (0, 16)
    nr0 = (15, 22) if up else (2, 9)
    nr1 = (15, 17) if up else (7, 9)
    nra = (13, 15) if up else (9, 11)
    nrb = (17, 20) if up else (4, 7)
    nw1 = near_window(up)
    if edge:
        lo_f = (7, 16) if up else (8, 17)
        fr0 = (8, 9) if up else (15, 16)
        fr1 = (8, 13) if up else (11, 16)
        hf = fr1
        fw1 = (6, 15) if up else (9, 18)
    else:
        lo_f = (0, 16) if up else (8, 24)
        fr0, fr0b = ((7, 9), (2, 7)) if up else ((15, 17), (17, 22))
        fr1 = fr0
        fra = (9, 11) if up else (13, 15)
        hf = (4, 11) if up else (13, 20)
        fw1 = far_window(up)

    cut = 2 * W_OVER
    SY.dma_start(out=T.vyi[:], in_=T.vy[:]).then_inc(sem.ldy, 16)
    SY.dma_start(out=T.vxi[:], in_=T.vx[:]).then_inc(sem.ldx, 16)
    SY.dma_start(out=T.pic[:, 1024:1024 + cut], in_=T.img[:, 0:cut]).then_inc(sem.ldi, 16)

    g.iota(out=T.pidx[:], pattern=[[1, 1]], base=0, channel_multiplier=1).then_inc(sem.gi, 1)
    g.iota(out=T.xiota[:], pattern=[[16, 4], [1, 16]], base=0, channel_multiplier=64).then_inc(sem.gi, 1)
    v(V.memset(T.jb[:, 0:512], 0.0), "msj")
    v(V.memset(T.sel[:], 128.0), "sb")
    v(V.memset(T.w0[:, 1024:2048], 0.0), "ms")
    S.wait_ge(sem.msj, 1)
    S.dma_start(out=T.pic[:, 1024 + cut:2048], in_=T.img[:, cut:1024]).then_inc(sem.ldj, 16)
    for c in (2048, 2560, 0, 512) if up else (0, 512, 2048, 2560):
        S.activation(out=T.w0[:, c:c + 512], in_=T.jb[:, 0:512], func=F.Copy).then_inc(sem.msh, 1)
    V.wait_ge(sem.gi, 2)
    v(ts(T.hi[:], T.pidx[:], 1, A.arith_shift_right, 7, A.bitwise_and))
    v(ts(T.oi[:], T.pidx[:], 4, A.arith_shift_right, 1, A.bitwise_and))
    if edge:
        v(ts(T.mi[:], T.pidx[:], 15, A.bitwise_and))
    xi, t1 = T.bp[:, 0:4, :], T.bp[:, 4:8, :]
    v(V.tensor_copy(out=xi, in_=T.xiota[:]))
    vs()
    v(ts(T.hrow[:], T.hi[:], float(8 * r + 8), A.add))
    v(ts(T.h128[:], T.hi[:], 128.0, A.mult, float(128 * (8 * r + 8)), A.add))
    v(ts(T.odd[:], T.oi[:], 1.0, A.mult))
    v(ts(T.even[:], T.oi[:], -1.0, A.mult, 1.0, A.add))
    vs()
    g.wait_ge(sem.sb, 1)
    pat = [[-16, 9], [1000, 16]]
    g.affine_select(T.sel[:], T.sel[:], pat, A.is_equal, 0.0, -15000, 1).then_inc(sem.sel1, 1)
    g.wait_ge(sem.sel1, 1)
    g.affine_select(T.sel[:], T.sel[:], pat, A.not_equal, 1.0, -15001, 1).then_inc(sem.sel2, 1)

    V.wait_ge(sem.ldy, 16)
    v(ts(T.dig[:, 0:4, :], T.vyi[:], T.hrow[:, 0:1], A.add), "dgr")
    V.wait_ge(sem.ldx, 16)
    v(V.tensor_tensor(out=T.ci[:], in0=T.vxi[:], in1=xi, op=A.add))
    vs()
    v(ts(T.ci[:], T.ci[:], 127, A.bitwise_and))
    v(ts(t1, T.vyi[:], 128.0, A.mult, T.h128[:, 0:1], A.add))
    vs()
    v(V.tensor_copy(out=T.dig[:, 4:8, :], in_=T.ci[:]), "dgc")
    v(V.tensor_tensor(out=T.gg[:], in0=t1, in1=T.ci[:], op=A.add))
    vs()
    v(ts(T.blk[:, :, 0:16], T.gg[:], T.even[:, 0:1], A.mult))
    v(ts(T.blk[:, :, 16:32], T.gg[:], T.odd[:, 0:1], A.mult))
    vs()
    for b in range(4):
        v(V.transpose(out=T.tb[:, b:128:4], in_=T.blk[:, b, :]))
    vs()
    v(V.tensor_tensor(out=T.lf[:], in0=T.tb[:, 0:64], in1=T.tb[:, 64:128], op=A.add))
    vs()
    for lst, d in ((T.lsf, fb), (T.lsn, nb)):
        if d is not None:
            first = 8 * T.rank_of(d) + (8 if r > T.rank_of(d) else 0)
            v(ts(lst[:], T.lf[:], -128.0 * first, A.add), "gd")
    low = (lo_f if up else lo_n)[0]
    v(ts(T.l0[:, 72:128], T.lf[:, 8:64], -128.0 * (top + 8), A.add), "lo")
    v(ts(T.l0[:, 64:72], T.lf[:, 0:8], -128.0 * (top + low), A.add), "lo")
    if edge:
        for k in range(1, 5):
            v(ts(T.kcol[:, k:k + 1], T.mi[:], 0.0, A.is_equal, float(-k if r == 0 else k), A.mult))
        vs()

    es = topo.engines(core, nb)
    ref = core if not edge else nb
    leave, stay = split(topo, ref, near[ref], over[(ref, far[ref])][0])
    sent = [0]

    def send(dst, to, src, engines, s):
        rid, pid = topo.addr(dst, core)
        g.remote_dma(to, src, s, sem.sent, pid, rid, bits(engines))
        sent[0] += len(engines)

    def fused(tr):
        g.remote_dma_fused(tr, local_sem=sem.sent)
        sent[0] += len(tr) * len(stay)

    def image(dst, to, a, b, engines, s):
        send(dst, to, T.pic[:, 1024 + a:1024 + b], engines, s)
    g.wait_ge(sem.dgr, 1)
    if not edge:
        send(out[(core, fb)][0], T.rvr[:], T.dig[:, 0:4, :], leave, sem.rvra)
    g.wait_ge(sem.dgc, 1)
    if not edge:
        send(out[(core, fb)][0], T.rvc[:], T.dig[:, 4:8, :], leave, sem.rvca)
    fused([transfer(topo, core, nb, T.dnr[:], T.dig[:, 0:4, :], stay, sem.vn),
           transfer(topo, core, nb, T.dnc[:], T.dig[:, 4:8, :], leave, sem.vn)])
    lc = list_column(T, core, nb)

    def lists(ready, name, here, there, at, a, b, relayed):
        g.wait_ge(sem[ready], 1 if edge else 2)
        tr = [transfer(topo, core, nb, at[:, a:b], here, stay, sem[name])]
        if not edge:
            tr.insert(0, transfer(topo, core, out[(core, fb)][0], relayed[0], there, leave, relayed[1]))
        fused(tr)
    lists("gd", "gvn", T.lsn[:], T.lsf[:], T.l0, lc, lc + 64, (T.rg[:], sem.rga))
    to = 0 if up else 2048
    g.wait_ge(sem.ldi, 16)
    second = ("gd1", "l1n", T.ln1[:], T.lf1[:], T.l1, lc + 8, lc + 56, (T.rh[:], sem.rha))
    if edge:
        g.wait_ge(sem.ldj, 16)
        g.wait_ge(sem.vn, len(es))
        image(nb, T.pic[:, to:to + 1024], 0, 1024, es, sem.pnr)
        lists(*second)
    else:
        ro, rw = out[(core, fb)], over[(core, fb)]
        image(rw[0], T.rq[:], *columns("over", 0), leave, sem.rpa)
        g.wait_ge(sem.ldj, 16)
        image(ro[0], T.rp[:], *columns("out", 0), stay, sem.rpa)
        g.wait_ge(sem.vn, len(es))
        image(rw[1], T.rq[:], *columns("over", 1), leave, sem.rpa)
        image(ro[1], T.rp[:], *columns("out", 1), stay, sem.rpa)
        lists(*second)
        g.wait_ge(sem.vfc, DIG_ENGINES)
        image(nb, T.pic[:, to:to + cut], 0, cut, stay, sem.pnr)
    pn_inc = len(es) if far.get(nb) is None else (1 + len(out[(nb, far[nb])])) * len(stay)

    def spread(q, h, src, col, name):
        q.dma_start(out=T.w0[h:128:16, col:col + 1024], in_=src).then_inc(sem[name], 16)
    ncol, fcol = (2048, 0) if up else (0, 2048)
    for h, q in enumerate((SY, S)):
        q.wait_ge(sem.ms, 1)
        q.wait_ge(sem.dgc if h else sem.dgr, 1)
        spread(q, h, T.dig[:, 4 * h:4 * h + 4, :], 1024, "rs_o")
    SY.wait_ge(sem.msh, 4)
    SY.wait_ge(sem.vn, len(es))
    spread(SY, 0, T.dnr[:], ncol, "rs_n")
    spread(SY, 1, T.dnc[:], ncol, "rs_n")
    if not edge:
        SY.wait_ge(sem.vfr, DIG_ENGINES)
        spread(SY, 0, T.dfr[:], fcol, "rs_f")
        SY.wait_ge(sem.vfc, DIG_ENGINES)
        spread(SY, 1, T.dfc[:], fcol, "rs_f")

    def part(eng, out, W, lst, a, b, d, name):
        o, i = out[:, 16 * (a - d):16 * (b - d)], W.indirect(lst[:, a:b])
        if eng is V:
            V.tensor_copy(out=o, in_=i).then_inc(sem[name], 1)
        else:
            S.activation(out=o, in_=i, func=F.Copy).then_inc(sem[name], 1)

    def gather(out, win, w, lst, rows, name, o0=0):
        a, b = 8 * rows[0], 8 * rows[1]
        m = a + (b - a) // 4 * 2
        part(V, out, win[:, 128 * w[0]:128 * w[1]], lst, a, m, 8 * o0, name)
        part(S, out, win[:, 128 * w[0]:128 * w[1]], lst, m, b, 8 * o0, name)

    def pick(ps, win, rows, name):
        a, b = 128 * rows[0], 128 * rows[1]
        k = (b - a) // 16
        for q in range(16):
            ins = TE.matmul(ps[:, 0:k], T.sel[:, 15 - q:143 - q], win[:, a + q:b:16], q == 0, q == 15)
        ins.then_inc(sem[name], 1)

    def both(name, k):
        V.wait_ge(sem[name], k)
        S.wait_ge(sem[name], k)

    def listed(lst, rows, ps, base, waits, name):
        V.wait_ge(sem[waits], 1)
        v(ts(lst[:, 8 * rows[0]:8 * rows[1]], ps[:, 0:8 * (rows[1] - rows[0])], -128.0 * (top + base), A.add), name)

    def beyond(win, ks, name):
        for k in ks:
            a, b = (8, 8 - k) if up else (15, 15 + k)
            v(ts(win[:, 128 * b:128 * b + 128], win[:, 128 * a:128 * a + 128], T.kcol[:, k:k + 1], A.add), name)

    V.wait_ge(sem.ms, 1)
    both("msh", 4)
    both("lo", 2)
    both("rs_o", 32)
    gather(T.w1, T.w0, (8, 16), T.l0, (9, 15), "g_e")
    TE.wait_ge(sem.sel2, 1)
    TE.wait_ge(sem.g_e, 2)
    pick(T.po, T.w1, (9, 15), "t_o")
    if edge:
        beyond(T.w0, (1,), "vir0")
        both("vir0", 1)
        gather(T.w1, T.w0, lo_f, T.l0, fr0, "g_f")
        TE.wait_ge(sem.g_f, 2)
        pick(T.pf, T.w1, fr1, "t_f")
        V.wait_ge(sem.g_f, 2)
        beyond(T.w1, (1, 2), "vir1")
    V.wait_ge(sem.t_o, 1)
    for lst, d, window in ((T.lf1, fb, far_window), (T.ln1, nb, near_window)):
        if d is not None:
            first = 8 * T.rank_of(d) + window(T.rank_of(near[d]) > T.rank_of(d))[0]
            v(ts(lst[:], T.po[:, 0:48], -128.0 * first, A.add), "gd1")
    own = [(nra, nw1[0])] if edge else [((11, 13), 9), (nra, nw1[0]), (fra, fw1[0])]
    for (a, b), base in own:
        v(ts(T.l1[:, 8 * a:8 * b], T.po[:, 8 * (a - 9):8 * (b - 9)], -128.0 * (top + base), A.add), "c_o")
    both("c_o", len(own))
    both("g_e", 2)
    if edge:
        both("vir1", 2)
        both("g_f", 2)
        listed(T.l1, fr1 if up else (11, 13), T.pf, fw1[0], "t_f", "c_f") if False else None
        V.wait_ge(sem.t_f, 1)
        v(ts(T.l3[:, 8 * fr1[0]:8 * fr1[1]], T.pf[:, 0:40], -128.0 * (top + fw1[0]), A.add), "c_f")
        both("c_f", 1)
        gather(T.w2, T.w1, fw1, T.l3, fr1, "h_f")
    else:
        gather(T.w2, T.w1, (9, 15), T.l1, (11, 13), "h_o")

    both("gvn", len(stay))
    both("rs_n", 32)
    gather(T.w1, T.w0, lo_n, T.l0, nr0, "g_n")
    TE.wait_ge(sem.g_n, 2)
    pick(T.pn, T.w1, nr1, "t_n")
    er, fr = ((12, 20), (4, 12)) if up else ((4, 12), (12, 20))
    ew = (8, 24) if up else (0, 16)
    if edge:
        V.wait_ge(sem.h_f, 2)
        beyond(T.w2, (1, 2, 3, 4), "vir2")
        TE.wait_ge(sem.h_f, 2)
        TE.wait_ge(sem.vir2, 4)
        both("ldi", 16)
        both("ldj", 16)
        a, b = (8, 0) if up else (15, 16)
        for k in range(8):
            v(V.tensor_copy(out=T.pic[:, 128 * (b + k):128 * (b + k) + 128], in_=T.pic[:, 128 * a:128 * a + 128]), "pv")
    both("g_n", 2)
    both("l1n", len(stay))
    if edge:
        gather(T.w2, T.w1, nw1, T.l1, nra, "h_m")
        gather(T.w2, T.w1, nw1, T.l1, nrb, "h_m")
        pick(T.p3, T.w2, fr, "t_3")
    else:
        gather(T.w2, T.w1, nw1, T.l1, nra, "h_m")
        gather(T.w2, T.w1, nw1, T.l1, nrb, "h_m")
        both("gvf", len(topo.engines(out[(fb, core)][0], core)))
        both("rs_f", 32)
        gather(T.w1, T.w0, lo_f, T.l0, fr0, "g_f")
        TE.wait_ge(sem.g_f, 2)
        pick(T.pf, T.w1, fr1, "t_f")
    listed(T.l1, nr1, T.pn, nw1[0], "t_n", "c_n")
    if not edge:
        gather(T.w1, T.w0, lo_f, T.l0, fr0b, "g_f2")
    both("c_n", 1)
    gather(T.w2, T.w1, nw1, T.l1, nr1, "h_n")
    if not edge:
        listed(T.l1, fr1, T.pf, fw1[0], "t_f", "c_f")
        both("c_f", 1)
        both("g_f", 2)
        both("g_f2", 2)
        both("l1f", len(topo.engines(out[(fb, core)][0], core)))
        gather(T.w2, T.w1, fw1, T.l1, hf, "h_f")

    TE.wait_ge(sem.h_f if edge else sem.h_o, 2)
    TE.wait_ge(sem.h_m, 4)
    TE.wait_ge(sem.h_n, 2)
    pick(T.p2, T.w2, er, "t_2")
    if edge:
        gw = (0, 16) if up else (8, 24)
        listed(T.l2e, fr, T.p3, gw[0], "t_3", "c_3")
        both("c_3", 1)
        both("pv", 8)
        gather(T.jb, T.pic, gw, T.l2e, fr, "g_j")
        v(ts(T.l2[:, 8 * fr[0]:8 * fr[1]], T.p3[:, 0:64], -128.0 * top, A.add), "c_2b")
    listed(T.l2e, er, T.p2, ew[0], "t_2", "c_2")
    both("c_2", 1)
    both("ldi", 16)
    both("ldj", 16)
    both("pnr", pn_inc)
    gather(T.jb, T.pic, ew, T.l2e, er, "g_2")
    if not edge:
        TE.wait_ge(sem.h_f, 2)
        pick(T.p3, T.w2, fr, "t_3")
        listed(T.l2, fr, T.p3, 0, "t_3", "c_3")
        both("c_3", 1)
        both("pfr", sum(len(topo.engines(x, core)) for x in out[(fb, core)] + over[(fb, core)]))
        gather(T.jb, T.pic, (0, 24), T.l2, fr, "g_j")
    v(ts(T.l2[:, 8 * er[0]:8 * er[1]], T.p2[:, 0:64], -128.0 * top, A.add), "c_2b")
    both("g_2", 2)
    both("g_j", 2)
    both("c_2b", 2 if edge else 1)
    both("msj", 1)
    gather(T.yo, T.jb, (0, 20), T.l2, (8, 12), "g_3a", 8)
    gather(T.yo, T.jb, (0, 20), T.l2, (12, 16), "g_3b", 8)
    SY.wait_ge(sem.g_3a, 2)
    SY.dma_start(out=T.y[:, 0:512], in_=T.yo[:, 0:512]).then_inc(sem.sty_a, 16)
    S.wait_ge(sem.g_3b, 2)
    S.dma_start(out=T.y[:, 512:1024], in_=T.yo[:, 512:1024]).then_inc(sem.sty_b, 16)
    g.wait_ge(sem.sent, sent[0])
    g.wait_ge(sem.sty_a, 16)
    g.wait_ge(sem.sty_b, 16)


def hand_on(g, core, T, topo, s, d, way, i, nb):
    sem = T.sem
    m, ne = topo.mask(core, d), len(topo.engines(core, d))
    es = topo.engines(s, core)
    a, b = columns(way, i)

    def pass_on(dst, to, held, arrived, mask):
        rid, pid = topo.addr(dst, core)
        g.remote_dma(to, held, arrived, sem.rsent, pid, rid, mask)

    def image(dst, held, arrived, mask):
        o = 0 if T.rank_of(dst) > T.rank_of(s) else 2048
        pass_on(dst, T.pic[:, o + a:o + b], held, arrived, mask)
    if way == "over":
        g.wait_ge(sem.rpa, len(es))
        image(d, T.rq[:], sem.pfr, m)
        g.wait_ge(sem.rsent, ne)
        return
    leave, stay = split(topo, core, nb, d)
    n = ne + len(stay)
    half = len(es) // 2
    lc = list_column(T, s, d)
    if i == 0:
        g.wait_ge(sem.rvra, half)
        pass_on(d, T.dfr[:], T.rvr[:], sem.vfr, bits(leave[:DIG_ENGINES]))
        g.wait_ge(sem.rvca, half)
        pass_on(d, T.dfc[:], T.rvc[:], sem.vfc, bits(leave[:DIG_ENGINES]))
        g.wait_ge(sem.rga, half)
        pass_on(d, T.l0[:, lc:lc + 64], T.rg[:], sem.gvf, m)
        n += 2 * DIG_ENGINES + 2 * ne
    g.wait_ge(sem.rpa, half)
    if i == 0:
        image(d, T.rp[:], sem.pfr, m)
    image(nb, T.rp[:], sem.pnr, bits(stay))
    if i == 0:
        g.wait_ge(sem.rha, half)
        pass_on(d, T.l1[:, lc + 8:lc + 56], T.rh[:], sem.l1f, m)
    else:
        image(d, T.rp[:], sem.pfr, m)
    g.wait_ge(sem.rsent, n)
